import numpy as np
import ml_dtypes


def mxq(x, axis, fmt="e4m3"):
    dtype, down = {"e4m3": (ml_dtypes.float8_e4m3fn, 7), "e5m2": (ml_dtypes.float8_e5m2, 14)}[fmt]
    v = np.moveaxis(np.asarray(x, np.float32).astype(ml_dtypes.bfloat16).astype(np.float64), axis, -1)
    blocks = v.reshape(v.shape[:-1] + (-1, 32))
    amax = np.abs(blocks).max(-1, keepdims=True)
    byte = np.maximum(np.where(amax > 0, np.frexp(amax)[1] - 1 + 127, 0) - down, 1)
    scale = np.exp2(byte - 127.0)
    codes = (blocks / scale).astype(np.float32).astype(dtype).astype(np.float64)
    return np.moveaxis((codes * scale).reshape(v.shape), -1, axis)


WIDE = False


def mx_kscale(k, group=512):
    if not WIDE:
        return np.ones(k)
    levels = np.array([10, -10, 5, -5, 0])
    if group != 512:
        return np.exp2(np.random.permutation(np.resize(levels, k // group))).repeat(group)
    if k % 512:
        return np.exp2(np.random.permutation(np.resize(levels, k // 32))).repeat(32)
    a = np.empty((k // 512, 16))
    for p in range(k // 512):
        a[p, :8] = np.random.permutation(np.resize(levels, 8))
        for g in range(8):
            far = levels[np.abs(levels - a[p, g]) >= 10]
            a[p, g + 8] = far[np.random.randint(len(far))]
    return np.exp2(a.ravel()).repeat(32)


def f64(x):
    return np.asarray(x).astype(np.float64)


def gelu(v):
    return 0.5 * v * (1.0 + np.tanh(0.7978845608028654 * (v + 0.044715 * v ** 3)))


G, D, K, M, N = 2, 256, 512, 256, 512


def setup_inputs():
    n = np.random.standard_normal
    s = mx_kscale(D, 0)[:, None]
    u = mx_kscale(K)[:, None]
    return {
        "x": (n((G, D, N)) * s).astype(np.float32),
        "w1": (n((G, D, K)) / np.sqrt(D) / s).astype(np.float32),
        "hs": (np.random.uniform(0.5, 2.0, (G, K, 1)) * u).astype(np.float32),
        "w2": (n((G, K, M)) / np.sqrt(K) / u).astype(np.float32),
    }


def reference(x, w1, hs, w2):
    xq = mxq(f64(x), 1, "e4m3")
    h = mxq(f64(w1), 1, "e4m3").transpose(0, 2, 1) @ xq
    h = (gelu(h)) * f64(hs)
    y = mxq(f64(w2), 1, "e4m3").transpose(0, 2, 1) @ mxq(h, 1, "e4m3")
    return y

@@ -1,0 +1,218 @@
+from contextlib import ExitStack
+
+import concourse.mybir as mybir
+
+G, D, K, M, N = 2, 256, 512, 256, 512
+FLOPS = 2 * G * N * (D * K + K * M)
+
+F32 = mybir.dt.float32
+BF16 = mybir.dt.bfloat16
+U32 = mybir.dt.uint32
+U8 = mybir.dt.uint8
+FP8X4 = mybir.dt.float8_e4m3fn_x4
+GELU = mybir.ActivationFunctionType.Gelu_apprx_tanh
+
+P = 128
+PACK = 4
+ROWS = D // PACK
+CW = 128
+CHUNKS = N // CW
+HALF = K // 2
+SH = HALF // PACK
+Z_BANKS = 2
+Y_BANKS = 4
+W1_SPLIT = 44
+
+
+def tile_rows_gmlp_gelu_kernel(tc, x, w1, hs, w2, out):
+    nc = tc.nc
+    with ExitStack() as ctx:
+        sb = ctx.enter_context(tc.tile_pool(name="sb", bufs=1))
+        ps = ctx.enter_context(tc.psum_pool(name="ps", bufs=1))
+
+        def tile(name, shape, dtype):
+            return sb.tile(shape, dtype, name=name, align_bytes=64)
+
+        x_raw = [tile("x_raw%d" % c, [P, PACK, CW], F32) for c in range(CHUNKS)]
+        x_bf = [tile("x_bf%d" % c, [P, CW, PACK], BF16) for c in range(CHUNKS)]
+        x_q = [tile("x_q%d" % c, [P, CW], U32) for c in range(CHUNKS)]
+        x_s = [tile("x_s%d" % c, [P, CW], U8) for c in range(CHUNKS)]
+        w1_raw = [tile("w1_raw%d" % h, [P, PACK, HALF], F32) for h in range(2)]
+        w1_bf = [tile("w1_bf%d" % h, [P, PACK, SH, PACK], BF16) for h in range(2)]
+        w1_q = [tile("w1_q%d" % r, [P, P], U32) for r in range(PACK)]
+        w1_s = [tile("w1_s%d" % r, [P, P], U8) for r in range(PACK)]
+        w2_raw = [tile("w2_raw%d" % g, [P, PACK, M], F32) for g in range(G)]
+        w2_bf = [tile("w2_bf%d" % g, [P, M, PACK], BF16) for g in range(G)]
+        w2_q = [tile("w2_q%d" % g, [P, M], U32) for g in range(G)]
+        w2_s = [tile("w2_s%d" % g, [P, M], U8) for g in range(G)]
+        hs_t = tile("hs_t", [P, G, 8], F32)
+        warm = tile("warm", [P, 2], F32)
+        units = [(c, g) for c in range(CHUNKS) for g in range(G)]
+        act = [tile("act%d" % u, [P, CW, PACK], F32) for u in range(len(units))]
+        h_bf = [tile("h_bf%d" % u, [P, CW, PACK], BF16) for u in range(len(units))]
+        h_q = [tile("h_q%d" % u, [P, CW], U32) for u in range(len(units))]
+        h_s = [tile("h_s%d" % u, [P, CW], U8) for u in range(len(units))]
+        y_sb = [tile("y_sb%d" % u, [P, 2, CW], F32) for u in range(len(units))]
+        z_ps = [[ps.tile([P, PACK, CW], F32, name="z_ps%d_%d" % (g, b)) for b in range(Z_BANKS)] for g in range(G)]
+        y_ps = [ps.tile([P, PACK, CW], F32, name="y_ps%d" % b) for b in range(Y_BANKS)]
+
+        x_v = x.rearrange("g (p j) n -> (g p) j n", j=PACK)
+        w1_v = w1.rearrange("g (p j) k -> (g p) j k", j=PACK)
+
+        def copy(eng, dst, src):
+            if eng == "S":
+                nc.scalar.copy(out=dst, in_=src)
+            else:
+                nc.vector.tensor_copy(out=dst, in_=src)
+
+        def load_x(c):
+            nc.sync.dma_start(out=x_raw[c][:], in_=x_v[:, :, c * CW:(c + 1) * CW])
+
+        def load_w1(h):
+            nc.sync.dma_start(out=w1_raw[h][:], in_=w1_v[:, :, h * HALF:(h + 1) * HALF])
+
+        def load_w2(g):
+            nc.sync.dma_start(out=w2_raw[g][:], in_=w2[g].rearrange("(p j) m -> p j m", j=PACK))
+
+        def interleave(eng, dst, src, lo, hi):
+            copy(eng,
+                 dst[:, lo:hi, :].rearrange("p (c i) j -> p c j i", i=4),
+                 src[:, :, lo:hi].rearrange("p j (c i) -> p c j i", i=4))
+
+        def cast_w1(eng, h, lo, hi):
+            copy(eng,
+                 w1_bf[h][:, :, lo:hi, :].rearrange("p r s j -> p s j r"),
+                 w1_raw[h][:, :, PACK * lo:PACK * hi].rearrange("p j (s r) -> p s j r", r=PACK))
+
+        def quant(codes, scales, src):
+            nc.vector.quantize_mx(out=codes.bitcast(FP8X4), scales=scales, in_=src)
+
+        def quant_w1(h, r):
+            quant(w1_q[r][:, h * SH:(h + 1) * SH], w1_s[r][:, h * SH:(h + 1) * SH],
+                  w1_bf[h][:, r].rearrange("p s j -> p (s j)"))
+
+        def quant_x(c):
+            quant(x_q[c][:], x_s[c][:], x_bf[c][:].rearrange("p n j -> p (n j)"))
+
+        def quant_w2(g):
+            quant(w2_q[g][:], w2_s[g][:], w2_bf[g][:].rearrange("p n j -> p (n j)"))
+
+        def mm1(c, g, r):
+            rows = slice(ROWS * g, ROWS * (g + 1))
+            nc.tensor.matmul_mx(
+                out=z_ps[g][c % Z_BANKS][:, r, :],
+                lhsT=w1_q[r][rows, :].bitcast(FP8X4), lhsT_scale=w1_s[r][rows, :],
+                rhs=x_q[c][rows, :].bitcast(FP8X4), rhs_scale=x_s[c][rows, :],
+                start=True, stop=True)
+
+        def layer1(c):
+            for r in range(PACK):
+                for g in range(G):
+                    mm1(c, g, r)
+
+        def gelu(u):
+            c, g = units[u]
+            nc.scalar.activation(out=act[u][:], in_=z_ps[g][c % Z_BANKS][:].rearrange("p r n -> p n r"), func=GELU)
+
+        def scale(u):
+            c, g = units[u]
+            nc.vector.tensor_tensor(
+                out=h_bf[u][:], in0=act[u][:],
+                in1=hs_t[:, g, 0:PACK].unsqueeze(1).to_broadcast([P, CW, PACK]),
+                op=mybir.AluOpType.mult)
+
+        def quant_h(u):
+            quant(h_q[u][:], h_s[u][:], h_bf[u][:].rearrange("p n j -> p (n j)"))
+
+        def layer2(u):
+            c, g = units[u]
+            for t in range(2):
+                cols = slice(t * P, (t + 1) * P)
+                nc.tensor.matmul_mx(
+                    out=y_ps[u % Y_BANKS][:, t, :],
+                    lhsT=w2_q[g][:, cols].bitcast(FP8X4), lhsT_scale=w2_s[g][:, cols],
+                    rhs=h_q[u][:].bitcast(FP8X4), rhs_scale=h_s[u][:],
+                    start=True, stop=True)
+
+        def finish(eng, u):
+            c, g = units[u]
+            copy(eng, y_sb[u][:], y_ps[u % Y_BANKS][:, 0:2, :])
+            nc.sync.dma_start(out=out[g].rearrange("(t p) n -> p t n", p=P)[:, :, c * CW:(c + 1) * CW], in_=y_sb[u][:])
+
+        with tc.manual_schedule():
+            load_x(0)
+            load_w1(0)
+            load_w1(1)
+            load_x(1)
+            load_x(2)
+            load_x(3)
+            load_w2(0)
+            load_w2(1)
+            nc.scalar.dma_start(out=hs_t[:, :, 0:PACK], in_=hs.rearrange("g (p r) o -> p g (r o)", r=PACK))
+            nc.gpsimd.memset(warm[:, 0:1], 0.0)
+            nc.scalar.activation(out=warm[:, 1:2], in_=warm[:, 0:1], func=GELU)
+            interleave("S", x_bf[0], x_raw[0], 0, CW)
+            cast_w1("V", 0, 0, SH)
+            quant_x(0)
+            for r in range(PACK):
+                quant_w1(0, r)
+            cast_w1("V", 1, 0, W1_SPLIT)
+            cast_w1("S", 1, W1_SPLIT, SH)
+            for r in range(PACK):
+                quant_w1(1, r)
+            interleave("S", x_bf[1], x_raw[1], 0, CW)
+            for g in range(G):
+                for r in range(PACK):
+                    mm1(0, g, r)
+            interleave("V", x_bf[2], x_raw[2], 0, CW)
+            quant_x(1)
+            layer1(1)
+            gelu(0)
+            gelu(1)
+            interleave("V", x_bf[3], x_raw[3], 0, CW)
+            quant_x(2)
+            scale(0)
+            quant_x(3)
+            layer1(2)
+            gelu(2)
+            gelu(3)
+            layer1(3)
+            interleave("V", w2_bf[0], w2_raw[0], 0, M)
+            scale(1)
+            quant_h(0)
+            quant_w2(0)
+            layer2(0)
+            gelu(4)
+            scale(2)
+            quant_h(1)
+            interleave("S", w2_bf[1], w2_raw[1], 0, M)
+            scale(3)
+            quant_h(2)
+            layer2(2)
+            scale(4)
+            quant_h(3)
+            quant_w2(1)
+            layer2(1)
+            layer2(3)
+            gelu(5)
+            finish("S",0)
+            quant_h(4)
+            layer2(4)
+            gelu(6)
+            finish("S",2)
+            scale(5)
+            gelu(7)
+            finish("S",1)
+            scale(6)
+            quant_h(5)
+            layer2(5)
+            finish("S",3)
+            finish("S",4)
+            scale(7)
+            quant_h(6)
+            layer2(6)
+            quant_h(7)
+            layer2(7)
+            finish("S",5)
+            finish("S",6)
+            finish("V",7)

@@ -16,12 +16,11 @@ P = 128
 PACK = 4
 ROWS = D // PACK
 CW = 128
-CHUNKS = N // CW
-HALF = K // 2
-SH = HALF // PACK
-Z_BANKS = 2
+PW = 2 * CW
+SH = P // 2
+W1_PIECES = [(0, 64), (64, 96), (96, 128)]
+X_PIECES = [(0, 128), (128, 256), (256, 384), (384, 512)]
 Y_BANKS = 4
-W1_SPLIT = 44
 
 
 def tile_rows_gmlp_gelu_kernel(tc, x, w1, hs, w2, out):
@@ -33,31 +32,31 @@ def tile_rows_gmlp_gelu_kernel(tc, x, w1, hs, w2, out):
         def tile(name, shape, dtype):
             return sb.tile(shape, dtype, name=name, align_bytes=64)
 
-        x_raw = [tile("x_raw%d" % c, [P, PACK, CW], F32) for c in range(CHUNKS)]
-        x_bf = [tile("x_bf%d" % c, [P, CW, PACK], BF16) for c in range(CHUNKS)]
-        x_q = [tile("x_q%d" % c, [P, CW], U32) for c in range(CHUNKS)]
-        x_s = [tile("x_s%d" % c, [P, CW], U8) for c in range(CHUNKS)]
-        w1_raw = [tile("w1_raw%d" % h, [P, PACK, HALF], F32) for h in range(2)]
+        x_raw = [tile("x_raw%d" % i, [P, PACK, hi - lo], F32) for i, (lo, hi) in enumerate(X_PIECES)]
+        x_bf = [tile("x_bf%d" % i, [P, hi - lo, PACK], BF16) for i, (lo, hi) in enumerate(X_PIECES)]
+        x_q = tile("x_q", [P, N], U32)
+        x_s = tile("x_s", [P, N], U8)
+        w1_raw = [tile("w1_raw%d" % i, [P, PACK, PACK * (hi - lo)], F32) for i, (lo, hi) in enumerate(W1_PIECES)]
         w1_bf = [tile("w1_bf%d" % h, [P, PACK, SH, PACK], BF16) for h in range(2)]
         w1_q = [tile("w1_q%d" % r, [P, P], U32) for r in range(PACK)]
         w1_s = [tile("w1_s%d" % r, [P, P], U8) for r in range(PACK)]
-        w2_raw = [tile("w2_raw%d" % g, [P, PACK, M], F32) for g in range(G)]
-        w2_bf = [tile("w2_bf%d" % g, [P, M, PACK], BF16) for g in range(G)]
-        w2_q = [tile("w2_q%d" % g, [P, M], U32) for g in range(G)]
-        w2_s = [tile("w2_s%d" % g, [P, M], U8) for g in range(G)]
+        w2_raw = [[tile("w2_raw%d_%d" % (g, t), [P, PACK, P], F32) for t in range(2)] for g in range(G)]
+        w2_bf = [[tile("w2_bf%d_%d" % (g, t), [P, P, PACK], BF16) for t in range(2)] for g in range(G)]
+        w2_q = [[tile("w2_q%d_%d" % (g, t), [P, P], U32) for t in range(2)] for g in range(G)]
+        w2_s = [[tile("w2_s%d_%d" % (g, t), [P, P], U8) for t in range(2)] for g in range(G)]
         hs_t = tile("hs_t", [P, G, 8], F32)
         warm = tile("warm", [P, 2], F32)
-        units = [(c, g) for c in range(CHUNKS) for g in range(G)]
-        act = [tile("act%d" % u, [P, CW, PACK], F32) for u in range(len(units))]
-        h_bf = [tile("h_bf%d" % u, [P, CW, PACK], BF16) for u in range(len(units))]
-        h_q = [tile("h_q%d" % u, [P, CW], U32) for u in range(len(units))]
-        h_s = [tile("h_s%d" % u, [P, CW], U8) for u in range(len(units))]
-        y_sb = [tile("y_sb%d" % u, [P, 2, CW], F32) for u in range(len(units))]
-        z_ps = [[ps.tile([P, PACK, CW], F32, name="z_ps%d_%d" % (g, b)) for b in range(Z_BANKS)] for g in range(G)]
-        y_ps = [ps.tile([P, PACK, CW], F32, name="y_ps%d" % b) for b in range(Y_BANKS)]
+        act = [tile("act%d" % g, [P, N, PACK], F32) for g in range(G)]
+        h_bf = [tile("h_bf%d" % g, [P, N, PACK], BF16) for g in range(G)]
+        h_q = [tile("h_q%d" % g, [P, N], U32) for g in range(G)]
+        h_s = [tile("h_s%d" % g, [P, N], U8) for g in range(G)]
+        y_sb = [[tile("y_sb%d_%d" % (g, q), [P, 2, PW], F32) for q in range(2)] for g in range(G)]
+        z_ps = [[ps.tile([P, PACK, CW], F32, name="z_ps%d_%d" % (g, b)) for b in range(2)] for g in range(G)]
+        y_ps = [ps.tile([P, 2, PW], F32, name="y_ps%d" % b) for b in range(Y_BANKS)]
 
         x_v = x.rearrange("g (p j) n -> (g p) j n", j=PACK)
         w1_v = w1.rearrange("g (p j) k -> (g p) j k", j=PACK)
+        out_v = out.rearrange("g (t p) n -> g p t n", p=P)
 
         def copy(eng, dst, src):
             if eng == "S":
@@ -65,154 +64,195 @@ def tile_rows_gmlp_gelu_kernel(tc, x, w1, hs, w2, out):
             else:
                 nc.vector.tensor_copy(out=dst, in_=src)
 
-        def load_x(c):
-            nc.sync.dma_start(out=x_raw[c][:], in_=x_v[:, :, c * CW:(c + 1) * CW])
+        def load_x(i):
+            lo, hi = X_PIECES[i]
+            nc.sync.dma_start(out=x_raw[i][:], in_=x_v[:, :, lo:hi])
 
-        def load_w1(h):
-            nc.sync.dma_start(out=w1_raw[h][:], in_=w1_v[:, :, h * HALF:(h + 1) * HALF])
+        def load_w1(i):
+            lo, hi = W1_PIECES[i]
+            nc.sync.dma_start(out=w1_raw[i][:], in_=w1_v[:, :, PACK * lo:PACK * hi])
 
-        def load_w2(g):
-            nc.sync.dma_start(out=w2_raw[g][:], in_=w2[g].rearrange("(p j) m -> p j m", j=PACK))
+        def load_w2(g, t):
+            nc.sync.dma_start(out=w2_raw[g][t][:], in_=w2[g].rearrange("(p j) m -> p j m", j=PACK)[:, :, t * P:(t + 1) * P])
+
+        def load_hs(q):
+            q.dma_start(out=hs_t[:, :, 0:PACK], in_=hs.rearrange("g (p r) o -> p g (r o)", r=PACK))
 
         def interleave(eng, dst, src, lo, hi):
             copy(eng,
                  dst[:, lo:hi, :].rearrange("p (c i) j -> p c j i", i=4),
                  src[:, :, lo:hi].rearrange("p j (c i) -> p c j i", i=4))
 
-        def cast_w1(eng, h, lo, hi):
+        def cast_x(eng, i, lo, hi):
+            interleave(eng, x_bf[i], x_raw[i], lo, hi)
+
+        def cast_w2(eng, g, t, lo, hi):
+            interleave(eng, w2_bf[g][t], w2_raw[g][t], lo, hi)
+
+        def cast_w1(eng, i, lo, hi):
+            first = W1_PIECES[i][0]
+            h = lo // SH
             copy(eng,
-                 w1_bf[h][:, :, lo:hi, :].rearrange("p r s j -> p s j r"),
-                 w1_raw[h][:, :, PACK * lo:PACK * hi].rearrange("p j (s r) -> p s j r", r=PACK))
+                 w1_bf[h][:, :, lo - h * SH:hi - h * SH, :].rearrange("p r s j -> p s j r"),
+                 w1_raw[i][:, :, PACK * (lo - first):PACK * (hi - first)].rearrange("p j (s r) -> p s j r", r=PACK))
 
         def quant(codes, scales, src):
             nc.vector.quantize_mx(out=codes.bitcast(FP8X4), scales=scales, in_=src)
 
-        def quant_w1(h, r):
-            quant(w1_q[r][:, h * SH:(h + 1) * SH], w1_s[r][:, h * SH:(h + 1) * SH],
-                  w1_bf[h][:, r].rearrange("p s j -> p (s j)"))
-
-        def quant_x(c):
-            quant(x_q[c][:], x_s[c][:], x_bf[c][:].rearrange("p n j -> p (n j)"))
-
-        def quant_w2(g):
-            quant(w2_q[g][:], w2_s[g][:], w2_bf[g][:].rearrange("p n j -> p (n j)"))
-
-        def mm1(c, g, r):
-            rows = slice(ROWS * g, ROWS * (g + 1))
-            nc.tensor.matmul_mx(
-                out=z_ps[g][c % Z_BANKS][:, r, :],
-                lhsT=w1_q[r][rows, :].bitcast(FP8X4), lhsT_scale=w1_s[r][rows, :],
-                rhs=x_q[c][rows, :].bitcast(FP8X4), rhs_scale=x_s[c][rows, :],
-                start=True, stop=True)
-
-        def layer1(c):
+        def quant_w1(h):
             for r in range(PACK):
-                for g in range(G):
-                    mm1(c, g, r)
+                quant(w1_q[r][:, h * SH:(h + 1) * SH], w1_s[r][:, h * SH:(h + 1) * SH],
+                      w1_bf[h][:, r].rearrange("p s j -> p (s j)"))
 
-        def gelu(u):
-            c, g = units[u]
-            nc.scalar.activation(out=act[u][:], in_=z_ps[g][c % Z_BANKS][:].rearrange("p r n -> p n r"), func=GELU)
+        def quant_x(i):
+            lo, hi = X_PIECES[i]
+            quant(x_q[:, lo:hi], x_s[:, lo:hi], x_bf[i][:].rearrange("p n j -> p (n j)"))
 
-        def scale(u):
-            c, g = units[u]
-            nc.vector.tensor_tensor(
-                out=h_bf[u][:], in0=act[u][:],
-                in1=hs_t[:, g, 0:PACK].unsqueeze(1).to_broadcast([P, CW, PACK]),
-                op=mybir.AluOpType.mult)
+        def quant_w2(g, t):
+            quant(w2_q[g][t][:], w2_s[g][t][:], w2_bf[g][t][:].rearrange("p n j -> p (n j)"))
 
-        def quant_h(u):
-            quant(h_q[u][:], h_s[u][:], h_bf[u][:].rearrange("p n j -> p (n j)"))
-
-        def layer2(u):
-            c, g = units[u]
-            for t in range(2):
-                cols = slice(t * P, (t + 1) * P)
+        def layer1(g, c):
+            rows = slice(ROWS * g, ROWS * (g + 1))
+            cols = slice(c * CW, (c + 1) * CW)
+            for r in range(PACK):
                 nc.tensor.matmul_mx(
-                    out=y_ps[u % Y_BANKS][:, t, :],
-                    lhsT=w2_q[g][:, cols].bitcast(FP8X4), lhsT_scale=w2_s[g][:, cols],
-                    rhs=h_q[u][:].bitcast(FP8X4), rhs_scale=h_s[u][:],
+                    out=z_ps[g][c % 2][:, r, :],
+                    lhsT=w1_q[r][rows, :].bitcast(FP8X4), lhsT_scale=w1_s[r][rows, :],
+                    rhs=x_q[rows, cols].bitcast(FP8X4), rhs_scale=x_s[rows, cols],
                     start=True, stop=True)
 
-        def finish(eng, u):
-            c, g = units[u]
-            copy(eng, y_sb[u][:], y_ps[u % Y_BANKS][:, 0:2, :])
-            nc.sync.dma_start(out=out[g].rearrange("(t p) n -> p t n", p=P)[:, :, c * CW:(c + 1) * CW], in_=y_sb[u][:])
+        def gelu(g, c):
+            nc.scalar.activation(out=act[g][:, c * CW:(c + 1) * CW, :],
+                                 in_=z_ps[g][c % 2][:].rearrange("p r n -> p n r"), func=GELU)
+
+        def scale(g, c, chunks=1):
+            cols = slice(c * CW, (c + chunks) * CW)
+            nc.vector.tensor_tensor(
+                out=h_bf[g][:, cols, :], in0=act[g][:, cols, :],
+                in1=hs_t[:, g, 0:PACK].unsqueeze(1).to_broadcast([P, chunks * CW, PACK]),
+                op=mybir.AluOpType.mult)
+
+        def quant_h(g, c, chunks=1):
+            cols = slice(c * CW, (c + chunks) * CW)
+            quant(h_q[g][:, cols], h_s[g][:, cols], h_bf[g][:, cols, :].rearrange("p n j -> p (n j)"))
+
+        def layer2(g, c, banks):
+            cols = slice(c * CW, (c + 1) * CW)
+            for t in range(2):
+                nc.tensor.matmul_mx(
+                    out=y_ps[banks[t]][:, t, (c % 2) * CW:(c % 2 + 1) * CW],
+                    lhsT=w2_q[g][t][:].bitcast(FP8X4), lhsT_scale=w2_s[g][t][:],
+                    rhs=h_q[g][:, cols].bitcast(FP8X4), rhs_scale=h_s[g][:, cols],
+                    start=True, stop=True)
+
+        def evac(eng, bank, g, c, chunks=1, t0=0, t1=2):
+            lo = (c % 2) * CW
+            copy(eng, y_sb[g][c // 2][:, t0:t1, lo:lo + chunks * CW], y_ps[bank][:, t0:t1, lo:lo + chunks * CW])
+
+        def store(q, g, c, chunks=1, t0=0, t1=2):
+            lo = (c % 2) * CW
+            q.dma_start(out=out_v[g][:, t0:t1, c * CW:(c + chunks) * CW],
+                        in_=y_sb[g][c // 2][:, t0:t1, lo:lo + chunks * CW])
 
         with tc.manual_schedule():
-            load_x(0)
             load_w1(0)
+            load_x(0)
             load_w1(1)
+            load_w1(2)
             load_x(1)
+            load_hs(nc.sync)
             load_x(2)
             load_x(3)
-            load_w2(0)
-            load_w2(1)
-            nc.scalar.dma_start(out=hs_t[:, :, 0:PACK], in_=hs.rearrange("g (p r) o -> p g (r o)", r=PACK))
+            load_w2(0,0)
+            load_w2(0,1)
+            load_w2(1,0)
+            load_w2(1,1)
             nc.gpsimd.memset(warm[:, 0:1], 0.0)
             nc.scalar.activation(out=warm[:, 1:2], in_=warm[:, 0:1], func=GELU)
-            interleave("S", x_bf[0], x_raw[0], 0, CW)
-            cast_w1("V", 0, 0, SH)
+            cast_w1("V",0,0,40)
+            cast_w1("S",0,40,64)
+            cast_x("S",0,0,64)
+            cast_x("V",0,64,128)
+            quant_w1(0)
+            cast_w1("V",1,64,84)
+            cast_w1("S",1,84,96)
             quant_x(0)
-            for r in range(PACK):
-                quant_w1(0, r)
-            cast_w1("V", 1, 0, W1_SPLIT)
-            cast_w1("S", 1, W1_SPLIT, SH)
-            for r in range(PACK):
-                quant_w1(1, r)
-            interleave("S", x_bf[1], x_raw[1], 0, CW)
-            for g in range(G):
-                for r in range(PACK):
-                    mm1(0, g, r)
-            interleave("V", x_bf[2], x_raw[2], 0, CW)
+            cast_w1("V",2,96,116)
+            cast_w1("S",2,116,128)
+            quant_w1(1)
+            layer1(0,0)
+            layer1(1,0)
+            cast_x("S",1,0,64)
+            cast_x("V",1,64,128)
+            cast_x("S",2,0,48)
+            cast_x("V",2,48,128)
             quant_x(1)
-            layer1(1)
-            gelu(0)
-            gelu(1)
-            interleave("V", x_bf[3], x_raw[3], 0, CW)
+            layer1(0,1)
+            layer1(1,1)
+            cast_x("V",3,0,128)
             quant_x(2)
-            scale(0)
+            gelu(0,0)
+            gelu(1,0)
+            cast_w2("V",0,0,0,64)
             quant_x(3)
-            layer1(2)
-            gelu(2)
-            gelu(3)
-            layer1(3)
-            interleave("V", w2_bf[0], w2_raw[0], 0, M)
-            scale(1)
-            quant_h(0)
-            quant_w2(0)
-            layer2(0)
-            gelu(4)
-            scale(2)
-            quant_h(1)
-            interleave("S", w2_bf[1], w2_raw[1], 0, M)
-            scale(3)
-            quant_h(2)
-            layer2(2)
-            scale(4)
-            quant_h(3)
-            quant_w2(1)
-            layer2(1)
-            layer2(3)
-            gelu(5)
-            finish("S",0)
-            quant_h(4)
-            layer2(4)
-            gelu(6)
-            finish("S",2)
-            scale(5)
-            gelu(7)
-            finish("S",1)
-            scale(6)
-            quant_h(5)
-            layer2(5)
-            finish("S",3)
-            finish("S",4)
-            scale(7)
-            quant_h(6)
-            layer2(6)
-            quant_h(7)
-            layer2(7)
-            finish("S",5)
-            finish("S",6)
-            finish("V",7)
+            scale(0,0)
+            layer1(0,2)
+            layer1(1,2)
+            gelu(0,1)
+            cast_w2("S",0,0,64,128)
+            gelu(1,1)
+            scale(1,0)
+            layer1(0,3)
+            layer1(1,3)
+            cast_w2("S",0,1,0,128)
+            scale(0,1)
+            quant_w2(0,0)
+            quant_h(0,0)
+            scale(1,1)
+            quant_w2(0,1)
+            quant_h(0,1)
+            layer2(0,0,(0,0))
+            layer2(0,1,(1,1))
+            gelu(0,2)
+            cast_w2("S",1,0,0,128)
+            gelu(1,2)
+            cast_w2("V",1,1,0,64)
+            scale(0,2)
+            quant_h(1,0)
+            cast_w2("S",1,1,64,128)
+            quant_h(1,1)
+            quant_w2(1,0)
+            scale(1,2)
+            quant_w2(1,1)
+            quant_h(0,2)
+            layer2(1,0,(2,2))
+            layer2(1,1,(3,3))
+            gelu(0,3)
+            evac("S",0,0,0)
+            store(nc.sync,0,0)
+            gelu(1,3)
+            evac("S",1,0,1)
+            store(nc.sync,0,1)
+            layer2(0,2,(0,0))
+            scale(0,3)
+            quant_h(1,2)
+            layer2(1,2,(1,1))
+            evac("S",2,1,0)
+            store(nc.sync,1,0)
+            quant_h(0,3)
+            evac("S",3,1,1)
+            store(nc.sync,1,1)
+            layer2(0,3,(2,2))
+            scale(1,3)
+            evac("S",0,0,2)
+            store(nc.sync,0,2)
+            evac("V",1,1,2)
+            store(nc.sync,1,2)
+            quant_h(1,3)
+            layer2(1,3,(3,0))
+            evac("S",2,0,3)
+            store(nc.sync,0,3)
+            evac("S",3,1,3,1,0,1)
+            evac("V",0,1,3,1,1,2)
+            store(nc.scalar,1,3,1,0,1)
+            store(nc.sync,1,3,1,1,2)

@@ -18,8 +18,8 @@ ROWS = D // PACK
 CW = 128
 PW = 2 * CW
 SH = P // 2
-W1_PIECES = [(0, 64), (64, 96), (96, 128)]
-X_PIECES = [(0, 128), (128, 256), (256, 384), (384, 512)]
+W1_PIECES = [(0, 128)]
+X_PIECES = [(0, 128), (128, 384), (384, 512)]
 Y_BANKS = 4
 
 
@@ -33,17 +33,17 @@ def tile_rows_gmlp_gelu_kernel(tc, x, w1, hs, w2, out):
             return sb.tile(shape, dtype, name=name, align_bytes=64)
 
         x_raw = [tile("x_raw%d" % i, [P, PACK, hi - lo], F32) for i, (lo, hi) in enumerate(X_PIECES)]
-        x_bf = [tile("x_bf%d" % i, [P, hi - lo, PACK], BF16) for i, (lo, hi) in enumerate(X_PIECES)]
+        x_bf = tile("x_bf", [P, N, PACK], BF16)
         x_q = tile("x_q", [P, N], U32)
         x_s = tile("x_s", [P, N], U8)
         w1_raw = [tile("w1_raw%d" % i, [P, PACK, PACK * (hi - lo)], F32) for i, (lo, hi) in enumerate(W1_PIECES)]
-        w1_bf = [tile("w1_bf%d" % h, [P, PACK, SH, PACK], BF16) for h in range(2)]
+        w1_bf = tile("w1_bf", [P, PACK, P, PACK], BF16)
         w1_q = [tile("w1_q%d" % r, [P, P], U32) for r in range(PACK)]
         w1_s = [tile("w1_s%d" % r, [P, P], U8) for r in range(PACK)]
-        w2_raw = [[tile("w2_raw%d_%d" % (g, t), [P, PACK, P], F32) for t in range(2)] for g in range(G)]
-        w2_bf = [[tile("w2_bf%d_%d" % (g, t), [P, P, PACK], BF16) for t in range(2)] for g in range(G)]
-        w2_q = [[tile("w2_q%d_%d" % (g, t), [P, P], U32) for t in range(2)] for g in range(G)]
-        w2_s = [[tile("w2_s%d_%d" % (g, t), [P, P], U8) for t in range(2)] for g in range(G)]
+        w2_raw = [tile("w2_raw%d" % g, [P, PACK, M], F32) for g in range(G)]
+        w2_bf = [tile("w2_bf%d" % g, [P, M, PACK], BF16) for g in range(G)]
+        w2_q = [tile("w2_q%d" % g, [P, M], U32) for g in range(G)]
+        w2_s = [tile("w2_s%d" % g, [P, M], U8) for g in range(G)]
         hs_t = tile("hs_t", [P, G, 8], F32)
         warm = tile("warm", [P, 2], F32)
         act = [tile("act%d" % g, [P, N, PACK], F32) for g in range(G)]
@@ -72,44 +72,39 @@ def tile_rows_gmlp_gelu_kernel(tc, x, w1, hs, w2, out):
             lo, hi = W1_PIECES[i]
             nc.sync.dma_start(out=w1_raw[i][:], in_=w1_v[:, :, PACK * lo:PACK * hi])
 
-        def load_w2(g, t):
-            nc.sync.dma_start(out=w2_raw[g][t][:], in_=w2[g].rearrange("(p j) m -> p j m", j=PACK)[:, :, t * P:(t + 1) * P])
+        def load_w2(g):
+            nc.sync.dma_start(out=w2_raw[g][:], in_=w2[g].rearrange("(p j) m -> p j m", j=PACK))
 
         def load_hs(q):
             q.dma_start(out=hs_t[:, :, 0:PACK], in_=hs.rearrange("g (p r) o -> p g (r o)", r=PACK))
 
-        def interleave(eng, dst, src, lo, hi):
-            copy(eng,
-                 dst[:, lo:hi, :].rearrange("p (c i) j -> p c j i", i=4),
-                 src[:, :, lo:hi].rearrange("p j (c i) -> p c j i", i=4))
+        def interleave(eng, dst, src):
+            copy(eng, dst.rearrange("p (c i) j -> p c j i", i=4), src.rearrange("p j (c i) -> p c j i", i=4))
 
         def cast_x(eng, i, lo, hi):
-            interleave(eng, x_bf[i], x_raw[i], lo, hi)
+            first = X_PIECES[i][0]
+            interleave(eng, x_bf[:, lo:hi, :], x_raw[i][:, :, lo - first:hi - first])
 
-        def cast_w2(eng, g, t, lo, hi):
-            interleave(eng, w2_bf[g][t], w2_raw[g][t], lo, hi)
+        def cast_w2(eng, g, lo, hi):
+            interleave(eng, w2_bf[g][:, lo:hi, :], w2_raw[g][:, :, lo:hi])
 
-        def cast_w1(eng, i, lo, hi):
-            first = W1_PIECES[i][0]
-            h = lo // SH
+        def cast_w1(eng, lo, hi):
             copy(eng,
-                 w1_bf[h][:, :, lo - h * SH:hi - h * SH, :].rearrange("p r s j -> p s j r"),
-                 w1_raw[i][:, :, PACK * (lo - first):PACK * (hi - first)].rearrange("p j (s r) -> p s j r", r=PACK))
+                 w1_bf[:, :, lo:hi, :].rearrange("p r s j -> p s j r"),
+                 w1_raw[0][:, :, PACK * lo:PACK * hi].rearrange("p j (s r) -> p s j r", r=PACK))
 
         def quant(codes, scales, src):
             nc.vector.quantize_mx(out=codes.bitcast(FP8X4), scales=scales, in_=src)
 
-        def quant_w1(h):
-            for r in range(PACK):
-                quant(w1_q[r][:, h * SH:(h + 1) * SH], w1_s[r][:, h * SH:(h + 1) * SH],
-                      w1_bf[h][:, r].rearrange("p s j -> p (s j)"))
+        def quant_w1(r):
+            quant(w1_q[r][:], w1_s[r][:], w1_bf[:, r].rearrange("p s j -> p (s j)"))
 
-        def quant_x(i):
-            lo, hi = X_PIECES[i]
-            quant(x_q[:, lo:hi], x_s[:, lo:hi], x_bf[i][:].rearrange("p n j -> p (n j)"))
+        def quant_x(c):
+            cols = slice(c * CW, (c + 1) * CW)
+            quant(x_q[:, cols], x_s[:, cols], x_bf[:, cols, :].rearrange("p n j -> p (n j)"))
 
-        def quant_w2(g, t):
-            quant(w2_q[g][t][:], w2_s[g][t][:], w2_bf[g][t][:].rearrange("p n j -> p (n j)"))
+        def quant_w2(g, lo=0, hi=M):
+            quant(w2_q[g][:, lo:hi], w2_s[g][:, lo:hi], w2_bf[g][:, lo:hi, :].rearrange("p n j -> p (n j)"))
 
         def layer1(g, c):
             rows = slice(ROWS * g, ROWS * (g + 1))
@@ -139,9 +134,10 @@ def tile_rows_gmlp_gelu_kernel(tc, x, w1, hs, w2, out):
         def layer2(g, c, banks):
             cols = slice(c * CW, (c + 1) * CW)
             for t in range(2):
+                ms = slice(t * P, (t + 1) * P)
                 nc.tensor.matmul_mx(
                     out=y_ps[banks[t]][:, t, (c % 2) * CW:(c % 2 + 1) * CW],
-                    lhsT=w2_q[g][t][:].bitcast(FP8X4), lhsT_scale=w2_s[g][t][:],
+                    lhsT=w2_q[g][:, ms].bitcast(FP8X4), lhsT_scale=w2_s[g][:, ms],
                     rhs=h_q[g][:, cols].bitcast(FP8X4), rhs_scale=h_s[g][:, cols],
                     start=True, stop=True)
 
@@ -157,102 +153,86 @@ def tile_rows_gmlp_gelu_kernel(tc, x, w1, hs, w2, out):
         with tc.manual_schedule():
             load_w1(0)
             load_x(0)
-            load_w1(1)
-            load_w1(2)
             load_x(1)
             load_hs(nc.sync)
             load_x(2)
-            load_x(3)
-            load_w2(0,0)
-            load_w2(0,1)
-            load_w2(1,0)
-            load_w2(1,1)
+            load_w2(0)
+            load_w2(1)
             nc.gpsimd.memset(warm[:, 0:1], 0.0)
             nc.scalar.activation(out=warm[:, 1:2], in_=warm[:, 0:1], func=GELU)
-            cast_w1("V",0,0,40)
-            cast_w1("S",0,40,64)
+            cast_w1("S",0,44)
+            cast_w1("V",44,128)
             cast_x("S",0,0,64)
             cast_x("V",0,64,128)
             quant_w1(0)
-            cast_w1("V",1,64,84)
-            cast_w1("S",1,84,96)
-            quant_x(0)
-            cast_w1("V",2,96,116)
-            cast_w1("S",2,116,128)
             quant_w1(1)
+            quant_x(0)
+            quant_w1(2)
+            quant_w1(3)
             layer1(0,0)
             layer1(1,0)
-            cast_x("S",1,0,64)
-            cast_x("V",1,64,128)
-            cast_x("S",2,0,48)
-            cast_x("V",2,48,128)
+            cast_x("S",1,128,192)
+            cast_x("V",1,192,256)
+            cast_x("V",1,256,384)
             quant_x(1)
             layer1(0,1)
             layer1(1,1)
-            cast_x("V",3,0,128)
             quant_x(2)
             gelu(0,0)
             gelu(1,0)
-            cast_w2("V",0,0,0,64)
-            quant_x(3)
+            cast_x("V",2,384,448)
+            cast_x("S",2,448,512)
             scale(0,0)
             layer1(0,2)
             layer1(1,2)
             gelu(0,1)
-            cast_w2("S",0,0,64,128)
-            gelu(1,1)
             scale(1,0)
+            quant_x(3)
             layer1(0,3)
+            cast_w2("S",0,0,128)
+            cast_w2("V",0,128,256)
+            gelu(1,1)
             layer1(1,3)
-            cast_w2("S",0,1,0,128)
             scale(0,1)
-            quant_w2(0,0)
             quant_h(0,0)
-            scale(1,1)
-            quant_w2(0,1)
-            quant_h(0,1)
+            quant_w2(0)
             layer2(0,0,(0,0))
-            layer2(0,1,(1,1))
             gelu(0,2)
-            cast_w2("S",1,0,0,128)
-            gelu(1,2)
-            cast_w2("V",1,1,0,64)
+            scale(1,1)
+            quant_h(0,1)
+            layer2(0,1,(0,0))
+            cast_w2("S",1,0,224)
+            cast_w2("V",1,224,256)
             scale(0,2)
-            quant_h(1,0)
-            cast_w2("S",1,1,64,128)
-            quant_h(1,1)
-            quant_w2(1,0)
-            scale(1,2)
-            quant_w2(1,1)
-            quant_h(0,2)
-            layer2(1,0,(2,2))
-            layer2(1,1,(3,3))
+            quant_h(1,0,2)
             gelu(0,3)
-            evac("S",0,0,0)
-            store(nc.sync,0,0)
-            gelu(1,3)
-            evac("S",1,0,1)
-            store(nc.sync,0,1)
-            layer2(0,2,(0,0))
+            quant_h(0,2)
+            layer2(0,2,(3,3))
+            quant_w2(1)
+            layer2(1,0,(1,1))
+            layer2(1,1,(2,2))
+            gelu(1,2)
             scale(0,3)
+            evac("S",0,0,0,2)
+            store(nc.sync,0,0,2)
+            scale(1,2)
+            quant_h(0,3)
+            layer2(0,3,(0,0))
+            gelu(1,3)
+            evac("V",1,1,0)
+            evac("S",2,1,1)
+            store(nc.sync,1,0,2)
             quant_h(1,2)
             layer2(1,2,(1,1))
-            evac("S",2,1,0)
-            store(nc.sync,1,0)
-            quant_h(0,3)
-            evac("S",3,1,1)
-            store(nc.sync,1,1)
-            layer2(0,3,(2,2))
             scale(1,3)
-            evac("S",0,0,2)
-            store(nc.sync,0,2)
-            evac("V",1,1,2)
-            store(nc.sync,1,2)
+            evac("S",3,0,2)
+            evac("S",0,0,3)
+            store(nc.sync,0,2,2)
             quant_h(1,3)
-            layer2(1,3,(3,0))
-            evac("S",2,0,3)
-            store(nc.sync,0,3)
-            evac("S",3,1,3,1,0,1)
-            evac("V",0,1,3,1,1,2)
+            layer2(1,3,(2,3))
+            evac("S",1,1,2)
+            store(nc.sync,1,2)
+            evac("S",2,1,3,1,0,1)
+            evac("V",3,1,3,1,1,2)
             store(nc.scalar,1,3,1,0,1)
             store(nc.sync,1,3,1,1,2)

@@ -88,10 +88,10 @@ def tile_rows_gmlp_gelu_kernel(tc, x, w1, hs, w2, out):
         def cast_w2(eng, g, lo, hi):
             interleave(eng, w2_bf[g][:, lo:hi, :], w2_raw[g][:, :, lo:hi])
 
-        def cast_w1(eng, lo, hi):
+        def cast_w1(eng, r0, lo, hi):
             copy(eng,
-                 w1_bf[:, :, lo:hi, :].rearrange("p r s j -> p s j r"),
-                 w1_raw[0][:, :, PACK * lo:PACK * hi].rearrange("p j (s r) -> p s j r", r=PACK))
+                 w1_bf[:, r0:r0 + 2, lo:hi, :].rearrange("p r s j -> p s j r"),
+                 w1_raw[0][:].rearrange("p j (s r) -> p s j r", r=PACK)[:, lo:hi, :, r0:r0 + 2])
 
         def quant(codes, scales, src):
             nc.vector.quantize_mx(out=codes.bitcast(FP8X4), scales=scales, in_=src)
@@ -154,20 +154,21 @@ def tile_rows_gmlp_gelu_kernel(tc, x, w1, hs, w2, out):
             load_w1(0)
             load_x(0)
             load_x(1)
-            load_hs(nc.sync)
             load_x(2)
             load_w2(0)
             load_w2(1)
+            load_hs(nc.scalar)
             nc.gpsimd.memset(warm[:, 0:1], 0.0)
             nc.scalar.activation(out=warm[:, 1:2], in_=warm[:, 0:1], func=GELU)
-            cast_w1("S",0,44)
-            cast_w1("V",44,128)
-            cast_x("S",0,0,64)
-            cast_x("V",0,64,128)
+            cast_w1("V",0,0,128)
+            cast_w1("S",2,0,32)
+            cast_w1("V",2,32,128)
+            cast_x("S",0,0,96)
+            cast_x("V",0,96,128)
             quant_w1(0)
             quant_w1(1)
-            quant_x(0)
             quant_w1(2)
+            quant_x(0)
             quant_w1(3)
             layer1(0,0)
             layer1(1,0)
@@ -180,8 +181,7 @@ def tile_rows_gmlp_gelu_kernel(tc, x, w1, hs, w2, out):
             quant_x(2)
             gelu(0,0)
             gelu(1,0)
-            cast_x("V",2,384,448)
-            cast_x("S",2,448,512)
+            cast_x("V",2,384,512)
             scale(0,0)
             layer1(0,2)
             layer1(1,2)
@@ -234,5 +234,5 @@ def tile_rows_gmlp_gelu_kernel(tc, x, w1, hs, w2, out):
             store(nc.sync,1,2)
             evac("S",2,1,3,1,0,1)
             evac("V",3,1,3,1,1,2)
-            store(nc.scalar,1,3,1,0,1)
+            store(nc.sync,1,3,1,0,1)
             store(nc.sync,1,3,1,1,2)

@@ -16,15 +16,14 @@ P = 128
 PACK = 4
 ROWS = D // PACK
 CW = 128
-PW = 2 * CW
-SH = P // 2
-W1_PIECES = [(0, 128)]
-X_PIECES = [(0, 128), (128, 384), (384, 512)]
-Y_BANKS = 4
+RUN = 4
+X_PIECES = [(0, 128), (128, 256), (256, 512)]
+STEPS = [(0, 0), (1, 0), (0, 1), (1, 1), (0, 2), (0, 3), (1, 2), (1, 3)]
 
 
 def tile_rows_gmlp_gelu_kernel(tc, x, w1, hs, w2, out):
     nc = tc.nc
+    V, S = nc.vector, nc.scalar
     with ExitStack() as ctx:
         sb = ctx.enter_context(tc.tile_pool(name="sb", bufs=1))
         ps = ctx.enter_context(tc.psum_pool(name="ps", bufs=1))
@@ -33,112 +32,116 @@ def tile_rows_gmlp_gelu_kernel(tc, x, w1, hs, w2, out):
             return sb.tile(shape, dtype, name=name, align_bytes=64)
 
         x_raw = [tile("x_raw%d" % i, [P, PACK, hi - lo], F32) for i, (lo, hi) in enumerate(X_PIECES)]
-        x_bf = tile("x_bf", [P, N, PACK], BF16)
+        x_bf = tile("x_bf", [P, N * PACK], BF16)
         x_q = tile("x_q", [P, N], U32)
         x_s = tile("x_s", [P, N], U8)
-        w1_raw = [tile("w1_raw%d" % i, [P, PACK, PACK * (hi - lo)], F32) for i, (lo, hi) in enumerate(W1_PIECES)]
-        w1_bf = tile("w1_bf", [P, PACK, P, PACK], BF16)
-        w1_q = [tile("w1_q%d" % r, [P, P], U32) for r in range(PACK)]
-        w1_s = [tile("w1_s%d" % r, [P, P], U8) for r in range(PACK)]
+        w1_raw = tile("w1_raw", [P, PACK, K], F32)
+        w1_bf = tile("w1_bf", [P, K * PACK], BF16)
+        w1_q = tile("w1_q", [P, K], U32)
+        w1_s = tile("w1_s", [P, K], U8)
         w2_raw = [tile("w2_raw%d" % g, [P, PACK, M], F32) for g in range(G)]
-        w2_bf = [tile("w2_bf%d" % g, [P, M, PACK], BF16) for g in range(G)]
+        w2_bf = [tile("w2_bf%d" % g, [P, M * PACK], BF16) for g in range(G)]
         w2_q = [tile("w2_q%d" % g, [P, M], U32) for g in range(G)]
         w2_s = [tile("w2_s%d" % g, [P, M], U8) for g in range(G)]
         hs_t = tile("hs_t", [P, G, 8], F32)
         warm = tile("warm", [P, 2], F32)
-        act = [tile("act%d" % g, [P, N, PACK], F32) for g in range(G)]
-        h_bf = [tile("h_bf%d" % g, [P, N, PACK], BF16) for g in range(G)]
-        h_q = [tile("h_q%d" % g, [P, N], U32) for g in range(G)]
-        h_s = [tile("h_s%d" % g, [P, N], U8) for g in range(G)]
-        y_sb = [[tile("y_sb%d_%d" % (g, q), [P, 2, PW], F32) for q in range(2)] for g in range(G)]
+        act = tile("act", [P, len(STEPS) * CW * PACK], F32)
+        h_bf = tile("h_bf", [P, len(STEPS) * CW * PACK], BF16)
+        h_q = tile("h_q", [P, len(STEPS) * CW], U32)
+        h_s = tile("h_s", [P, len(STEPS) * CW], U8)
+        y_sb = [[tile("y_sb%d_%d" % (g, q), [P, 2, 2 * CW], F32) for q in range(2)] for g in range(G)]
         z_ps = [[ps.tile([P, PACK, CW], F32, name="z_ps%d_%d" % (g, b)) for b in range(2)] for g in range(G)]
-        y_ps = [ps.tile([P, 2, PW], F32, name="y_ps%d" % b) for b in range(Y_BANKS)]
+        y_ps = [ps.tile([P, 2, 2 * CW], F32, name="y_ps%d" % b) for b in range(4)]
 
         x_v = x.rearrange("g (p j) n -> (g p) j n", j=PACK)
         w1_v = w1.rearrange("g (p j) k -> (g p) j k", j=PACK)
         out_v = out.rearrange("g (t p) n -> g p t n", p=P)
 
         def copy(eng, dst, src):
-            if eng == "S":
-                nc.scalar.copy(out=dst, in_=src)
+            if eng is S:
+                S.copy(out=dst, in_=src)
             else:
-                nc.vector.tensor_copy(out=dst, in_=src)
+                V.tensor_copy(out=dst, in_=src)
 
-        def load_x(i):
+        def load_x(i, q=nc.sync):
             lo, hi = X_PIECES[i]
-            nc.sync.dma_start(out=x_raw[i][:], in_=x_v[:, :, lo:hi])
+            q.dma_start(out=x_raw[i][:], in_=x_v[:, :, lo:hi])
 
-        def load_w1(i):
-            lo, hi = W1_PIECES[i]
-            nc.sync.dma_start(out=w1_raw[i][:], in_=w1_v[:, :, PACK * lo:PACK * hi])
-
-        def load_w2(g):
-            nc.sync.dma_start(out=w2_raw[g][:], in_=w2[g].rearrange("(p j) m -> p j m", j=PACK))
+        def load_w2(g, q=nc.sync):
+            q.dma_start(out=w2_raw[g][:], in_=w2[g].rearrange("(p j) m -> p j m", j=PACK))
 
         def load_hs(q):
             q.dma_start(out=hs_t[:, :, 0:PACK], in_=hs.rearrange("g (p r) o -> p g (r o)", r=PACK))
 
         def interleave(eng, dst, src):
-            copy(eng, dst.rearrange("p (c i) j -> p c j i", i=4), src.rearrange("p j (c i) -> p c j i", i=4))
+            copy(eng, dst.rearrange("p (c i j) -> p c j i", i=RUN, j=PACK),
+                 src.rearrange("p j (c i) -> p c j i", i=RUN))
 
-        def cast_x(eng, i, lo, hi):
+        def cast_x(eng, lo, hi):
+            i = max(i for i, piece in enumerate(X_PIECES) if piece[0] <= lo)
             first = X_PIECES[i][0]
-            interleave(eng, x_bf[:, lo:hi, :], x_raw[i][:, :, lo - first:hi - first])
+            interleave(eng, x_bf[:, PACK * lo:PACK * hi], x_raw[i][:, :, lo - first:hi - first])
 
         def cast_w2(eng, g, lo, hi):
-            interleave(eng, w2_bf[g][:, lo:hi, :], w2_raw[g][:, :, lo:hi])
+            interleave(eng, w2_bf[g][:, PACK * lo:PACK * hi], w2_raw[g][:, :, lo:hi])
 
-        def cast_w1(eng, r0, lo, hi):
+        def cast_w1(eng, r0, r1, lo, hi):
             copy(eng,
-                 w1_bf[:, r0:r0 + 2, lo:hi, :].rearrange("p r s j -> p s j r"),
-                 w1_raw[0][:].rearrange("p j (s r) -> p s j r", r=PACK)[:, lo:hi, :, r0:r0 + 2])
+                 w1_bf[:].rearrange("p (r s j) -> p s j r", r=PACK, j=PACK)[:, lo:hi, :, r0:r1],
+                 w1_raw[:].rearrange("p j (s r) -> p s j r", r=PACK)[:, lo:hi, :, r0:r1])
 
-        def quant(codes, scales, src):
-            nc.vector.quantize_mx(out=codes.bitcast(FP8X4), scales=scales, in_=src)
+        def quant(codes, scales, src, lo, hi):
+            V.quantize_mx(out=codes[:, lo:hi].bitcast(FP8X4), scales=scales[:, lo:hi],
+                          in_=src[:, PACK * lo:PACK * hi])
 
-        def quant_w1(r):
-            quant(w1_q[r][:], w1_s[r][:], w1_bf[:, r].rearrange("p s j -> p (s j)"))
+        def quant_w1(r0, r1):
+            quant(w1_q, w1_s, w1_bf, r0 * P, r1 * P)
 
-        def quant_x(c):
-            cols = slice(c * CW, (c + 1) * CW)
-            quant(x_q[:, cols], x_s[:, cols], x_bf[:, cols, :].rearrange("p n j -> p (n j)"))
+        def quant_x(c0, c1):
+            quant(x_q, x_s, x_bf, c0 * CW, c1 * CW)
 
-        def quant_w2(g, lo=0, hi=M):
-            quant(w2_q[g][:, lo:hi], w2_s[g][:, lo:hi], w2_bf[g][:, lo:hi, :].rearrange("p n j -> p (n j)"))
+        def quant_w2(g):
+            quant(w2_q[g], w2_s[g], w2_bf[g], 0, M)
 
-        def layer1(g, c):
+        def quant_h(u0, u1):
+            quant(h_q, h_s, h_bf, u0 * CW, u1 * CW)
+
+        def layer1(u, r0=0, r1=PACK):
+            g, c = STEPS[u]
             rows = slice(ROWS * g, ROWS * (g + 1))
             cols = slice(c * CW, (c + 1) * CW)
-            for r in range(PACK):
+            for r in range(r0, r1):
+                ks = slice(r * P, (r + 1) * P)
                 nc.tensor.matmul_mx(
                     out=z_ps[g][c % 2][:, r, :],
-                    lhsT=w1_q[r][rows, :].bitcast(FP8X4), lhsT_scale=w1_s[r][rows, :],
+                    lhsT=w1_q[rows, ks].bitcast(FP8X4), lhsT_scale=w1_s[rows, ks],
                     rhs=x_q[rows, cols].bitcast(FP8X4), rhs_scale=x_s[rows, cols],
                     start=True, stop=True)
 
-        def gelu(g, c):
-            nc.scalar.activation(out=act[g][:, c * CW:(c + 1) * CW, :],
-                                 in_=z_ps[g][c % 2][:].rearrange("p r n -> p n r"), func=GELU)
+        def gelu(u):
+            g, c = STEPS[u]
+            S.activation(out=act[:, u * CW * PACK:(u + 1) * CW * PACK].rearrange("p (n r) -> p n r", r=PACK),
+                         in_=z_ps[g][c % 2][:].rearrange("p r n -> p n r"), func=GELU)
 
-        def scale(g, c, chunks=1):
-            cols = slice(c * CW, (c + chunks) * CW)
-            nc.vector.tensor_tensor(
-                out=h_bf[g][:, cols, :], in0=act[g][:, cols, :],
-                in1=hs_t[:, g, 0:PACK].unsqueeze(1).to_broadcast([P, chunks * CW, PACK]),
+        def scale(u0, u1):
+            g0, g1 = STEPS[u0][0], STEPS[u1 - 1][0] + 1
+            span = slice(u0 * CW * PACK, u1 * CW * PACK)
+            width = (u1 - u0) * CW // (g1 - g0)
+            V.tensor_tensor(
+                out=h_bf[:, span].rearrange("p (g n r) -> p g n r", g=g1 - g0, r=PACK),
+                in0=act[:, span].rearrange("p (g n r) -> p g n r", g=g1 - g0, r=PACK),
+                in1=hs_t[:, g0:g1, 0:PACK].unsqueeze(2).to_broadcast([P, g1 - g0, width, PACK]),
                 op=mybir.AluOpType.mult)
 
-        def quant_h(g, c, chunks=1):
-            cols = slice(c * CW, (c + chunks) * CW)
-            quant(h_q[g][:, cols], h_s[g][:, cols], h_bf[g][:, cols, :].rearrange("p n j -> p (n j)"))
-
-        def layer2(g, c, banks):
-            cols = slice(c * CW, (c + 1) * CW)
+        def layer2(u, banks):
+            g, c = STEPS[u]
+            cols = slice(u * CW, (u + 1) * CW)
             for t in range(2):
                 ms = slice(t * P, (t + 1) * P)
                 nc.tensor.matmul_mx(
                     out=y_ps[banks[t]][:, t, (c % 2) * CW:(c % 2 + 1) * CW],
                     lhsT=w2_q[g][:, ms].bitcast(FP8X4), lhsT_scale=w2_s[g][:, ms],
-                    rhs=h_q[g][:, cols].bitcast(FP8X4), rhs_scale=h_s[g][:, cols],
+                    rhs=h_q[:, cols].bitcast(FP8X4), rhs_scale=h_s[:, cols],
                     start=True, stop=True)
 
         def evac(eng, bank, g, c, chunks=1, t0=0, t1=2):
@@ -151,88 +154,78 @@ def tile_rows_gmlp_gelu_kernel(tc, x, w1, hs, w2, out):
                         in_=y_sb[g][c // 2][:, t0:t1, lo:lo + chunks * CW])
 
         with tc.manual_schedule():
-            load_w1(0)
+            nc.sync.dma_start(out=w1_raw[:], in_=w1_v)
             load_x(0)
+            load_w2(0)
             load_x(1)
             load_x(2)
-            load_w2(0)
             load_w2(1)
             load_hs(nc.scalar)
             nc.gpsimd.memset(warm[:, 0:1], 0.0)
-            nc.scalar.activation(out=warm[:, 1:2], in_=warm[:, 0:1], func=GELU)
-            cast_w1("V",0,0,128)
-            cast_w1("S",2,0,32)
-            cast_w1("V",2,32,128)
-            cast_x("S",0,0,96)
-            cast_x("V",0,96,128)
-            quant_w1(0)
-            quant_w1(1)
-            quant_w1(2)
-            quant_x(0)
-            quant_w1(3)
-            layer1(0,0)
-            layer1(1,0)
-            cast_x("S",1,128,192)
-            cast_x("V",1,192,256)
-            cast_x("V",1,256,384)
-            quant_x(1)
-            layer1(0,1)
-            layer1(1,1)
-            quant_x(2)
-            gelu(0,0)
-            gelu(1,0)
-            cast_x("V",2,384,512)
-            scale(0,0)
-            layer1(0,2)
-            layer1(1,2)
-            gelu(0,1)
-            scale(1,0)
-            quant_x(3)
-            layer1(0,3)
-            cast_w2("S",0,0,128)
-            cast_w2("V",0,128,256)
-            gelu(1,1)
-            layer1(1,3)
-            scale(0,1)
-            quant_h(0,0)
+            S.activation(out=warm[:, 1:2], in_=warm[:, 0:1], func=GELU)
+            cast_w1(V, 0, 2, 0, 128)
+            cast_w1(S, 2, 4, 0, 80)
+            cast_w1(V, 2, 4, 80, 128)
+            cast_x(S, 0, 128)
+            quant_w1(0, 2)
+            quant_w1(2, 4)
+            quant_x(0, 1)
+            layer1(0)
+            layer1(1)
+            cast_w2(S, 0, 0, 128)
+            cast_w2(V, 0, 128, 256)
+            cast_x(V, 128, 256)
             quant_w2(0)
-            layer2(0,0,(0,0))
-            gelu(0,2)
-            scale(1,1)
-            quant_h(0,1)
-            layer2(0,1,(0,0))
-            cast_w2("S",1,0,224)
-            cast_w2("V",1,224,256)
-            scale(0,2)
-            quant_h(1,0,2)
-            gelu(0,3)
-            quant_h(0,2)
-            layer2(0,2,(3,3))
+            quant_x(1, 2)
+            layer1(2)
+            layer1(3)
+            gelu(0)
+            gelu(1)
+            scale(0, 1)
+            cast_x(S, 256, 384)
+            cast_x(V, 384, 512)
+            scale(1, 2)
+            quant_x(2, 4)
+            gelu(2)
+            gelu(3)
+            layer1(4)
+            layer1(5)
+            layer1(6)
+            layer1(7)
+            quant_h(0, 2)
+            layer2(0, (0, 0))
+            scale(2, 3)
+            cast_w2(S, 1, 0, 192)
+            cast_w2(V, 1, 192, 256)
+            scale(3, 4)
+            gelu(4)
+            gelu(5)
+            quant_h(2, 3)
+            layer2(2, (0, 0))
             quant_w2(1)
-            layer2(1,0,(1,1))
-            layer2(1,1,(2,2))
-            gelu(1,2)
-            scale(0,3)
-            evac("S",0,0,0,2)
-            store(nc.sync,0,0,2)
-            scale(1,2)
-            quant_h(0,3)
-            layer2(0,3,(0,0))
-            gelu(1,3)
-            evac("V",1,1,0)
-            evac("S",2,1,1)
-            store(nc.sync,1,0,2)
-            quant_h(1,2)
-            layer2(1,2,(1,1))
-            scale(1,3)
-            evac("S",3,0,2)
-            evac("S",0,0,3)
-            store(nc.sync,0,2,2)
-            quant_h(1,3)
-            layer2(1,3,(2,3))
-            evac("S",1,1,2)
-            store(nc.sync,1,2)
-            evac("S",2,1,3,1,0,1)
-            evac("V",3,1,3,1,1,2)
-            store(nc.sync,1,3,1,0,1)
-            store(nc.sync,1,3,1,1,2)
+            quant_h(3, 4)
+            layer2(1, (1, 1))
+            layer2(3, (1, 1))
+            scale(4, 6)
+            gelu(6)
+            gelu(7)
+            evac(S, 0, 0, 0, 2)
+            store(nc.sync, 0, 0, 2)
+            evac(S, 1, 1, 0, 2)
+            store(nc.sync, 1, 0, 2)
+            scale(6, 7)
+            quant_h(4, 6)
+            layer2(4, (2, 2))
+            layer2(5, (2, 2))
+            scale(7, 8)
+            quant_h(6, 7)
+            layer2(6, (3, 3))
+            quant_h(7, 8)
+            layer2(7, (0, 1))
+            evac(S, 2, 0, 2, 2)
+            store(nc.sync, 0, 2, 2)
+            evac(V, 3, 1, 2)
+            store(nc.sync, 1, 2)
+            evac(V, 1, 1, 3, 1, 1, 2)
+            evac(S, 0, 1, 3, 1, 0, 1)
+            store(nc.sync, 1, 3)

@@ -16,8 +16,8 @@ P = 128
 PACK = 4
 ROWS = D // PACK
 CW = 128
-RUN = 4
-X_PIECES = [(0, 128), (128, 256), (256, 512)]
+RUN = 2
+X_PIECES = [(0, 128), (128, 384), (384, 512)]
 STEPS = [(0, 0), (1, 0), (0, 1), (1, 1), (0, 2), (0, 3), (1, 2), (1, 3)]
 
 
@@ -35,7 +35,7 @@ def tile_rows_gmlp_gelu_kernel(tc, x, w1, hs, w2, out):
         x_bf = tile("x_bf", [P, N * PACK], BF16)
         x_q = tile("x_q", [P, N], U32)
         x_s = tile("x_s", [P, N], U8)
-        w1_raw = tile("w1_raw", [P, PACK, K], F32)
+        w1_raw = [tile("w1_raw%d" % i, [P, 2, K], F32) for i in range(2)]
         w1_bf = tile("w1_bf", [P, K * PACK], BF16)
         w1_q = tile("w1_q", [P, K], U32)
         w1_s = tile("w1_s", [P, K], U8)
@@ -67,6 +67,9 @@ def tile_rows_gmlp_gelu_kernel(tc, x, w1, hs, w2, out):
             lo, hi = X_PIECES[i]
             q.dma_start(out=x_raw[i][:], in_=x_v[:, :, lo:hi])
 
+        def load_w1(i, q=nc.sync):
+            q.dma_start(out=w1_raw[i][:], in_=w1_v[:, 2 * i:2 * i + 2, :])
+
         def load_w2(g, q=nc.sync):
             q.dma_start(out=w2_raw[g][:], in_=w2[g].rearrange("(p j) m -> p j m", j=PACK))
 
@@ -85,10 +88,10 @@ def tile_rows_gmlp_gelu_kernel(tc, x, w1, hs, w2, out):
         def cast_w2(eng, g, lo, hi):
             interleave(eng, w2_bf[g][:, PACK * lo:PACK * hi], w2_raw[g][:, :, lo:hi])
 
-        def cast_w1(eng, r0, r1, lo, hi):
+        def cast_w1(eng, r0, r1, lo, hi, j0, j1):
             copy(eng,
-                 w1_bf[:].rearrange("p (r s j) -> p s j r", r=PACK, j=PACK)[:, lo:hi, :, r0:r1],
-                 w1_raw[:].rearrange("p j (s r) -> p s j r", r=PACK)[:, lo:hi, :, r0:r1])
+                 w1_bf[:].rearrange("p (r s j) -> p s j r", r=PACK, j=PACK)[:, lo:hi, j0:j1, r0:r1],
+                 w1_raw[j0 // 2][:].rearrange("p j (s r) -> p s j r", r=PACK)[:, lo:hi, :, r0:r1])
 
         def quant(codes, scales, src, lo, hi):
             V.quantize_mx(out=codes[:, lo:hi].bitcast(FP8X4), scales=scales[:, lo:hi],
@@ -154,78 +157,84 @@ def tile_rows_gmlp_gelu_kernel(tc, x, w1, hs, w2, out):
                         in_=y_sb[g][c // 2][:, t0:t1, lo:lo + chunks * CW])
 
         with tc.manual_schedule():
-            nc.sync.dma_start(out=w1_raw[:], in_=w1_v)
+            load_w1(0)
+            load_w1(1)
             load_x(0)
-            load_w2(0)
             load_x(1)
             load_x(2)
+            load_w2(0)
             load_w2(1)
             load_hs(nc.scalar)
             nc.gpsimd.memset(warm[:, 0:1], 0.0)
             S.activation(out=warm[:, 1:2], in_=warm[:, 0:1], func=GELU)
-            cast_w1(V, 0, 2, 0, 128)
-            cast_w1(S, 2, 4, 0, 80)
-            cast_w1(V, 2, 4, 80, 128)
-            cast_x(S, 0, 128)
+            cast_w1(S, 2, 4, 0, 64, 2, 4)
+            cast_w1(V, 0, 4, 0, 128, 0, 2)
+            cast_x(S, 0, 64)
+            cast_w1(V, 0, 2, 0, 128, 2, 4)
+            cast_x(S, 256, 320)
+            cast_w1(V, 2, 4, 64, 128, 2, 4)
+            cast_x(V, 64, 128)
             quant_w1(0, 2)
-            quant_w1(2, 4)
             quant_x(0, 1)
-            layer1(0)
-            layer1(1)
-            cast_w2(S, 0, 0, 128)
-            cast_w2(V, 0, 128, 256)
+            layer1(0, 0, 2)
+            layer1(1, 0, 2)
+            quant_w1(2, 4)
+            layer1(0, 2, 4)
+            layer1(1, 2, 4)
+            gelu(0)
             cast_x(V, 128, 256)
-            quant_w2(0)
+            gelu(1)
+            cast_x(V, 320, 384)
             quant_x(1, 2)
             layer1(2)
             layer1(3)
-            gelu(0)
-            gelu(1)
-            scale(0, 1)
-            cast_x(S, 256, 384)
-            cast_x(V, 384, 512)
-            scale(1, 2)
-            quant_x(2, 4)
             gelu(2)
+            cast_x(V, 384, 512)
             gelu(3)
+            quant_x(2, 3)
             layer1(4)
+            cast_w2(S, 0, 0, 160)
+            scale(0, 1)
+            gelu(4)
+            quant_x(3, 4)
             layer1(5)
             layer1(6)
             layer1(7)
-            quant_h(0, 2)
-            layer2(0, (0, 0))
-            scale(2, 3)
             cast_w2(S, 1, 0, 192)
-            cast_w2(V, 1, 192, 256)
-            scale(3, 4)
-            gelu(4)
+            scale(1, 2)
             gelu(5)
-            quant_h(2, 3)
+            cast_w2(V, 0, 160, 256)
+            gelu(6)
+            scale(2, 3)
+            scale(3, 4)
+            quant_w2(0)
+            quant_h(0, 4)
+            layer2(0, (0, 0))
             layer2(2, (0, 0))
+            evac(S, 0, 0, 0, 2)
+            cast_w2(V, 1, 192, 256)
+            store(nc.sync, 0, 0, 2)
+            gelu(7)
+            scale(4, 5)
             quant_w2(1)
-            quant_h(3, 4)
             layer2(1, (1, 1))
             layer2(3, (1, 1))
-            scale(4, 6)
-            gelu(6)
-            gelu(7)
-            evac(S, 0, 0, 0, 2)
-            store(nc.sync, 0, 0, 2)
             evac(S, 1, 1, 0, 2)
+            scale(5, 6)
             store(nc.sync, 1, 0, 2)
-            scale(6, 7)
-            quant_h(4, 6)
+            quant_h(4, 5)
             layer2(4, (2, 2))
+            scale(6, 7)
+            quant_h(5, 6)
             layer2(5, (2, 2))
-            scale(7, 8)
-            quant_h(6, 7)
-            layer2(6, (3, 3))
-            quant_h(7, 8)
-            layer2(7, (0, 1))
             evac(S, 2, 0, 2, 2)
+            scale(7, 8)
             store(nc.sync, 0, 2, 2)
-            evac(V, 3, 1, 2)
-            store(nc.sync, 1, 2)
-            evac(V, 1, 1, 3, 1, 1, 2)
-            evac(S, 0, 1, 3, 1, 0, 1)
-            store(nc.sync, 1, 3)
+            quant_h(6, 7)
+            layer2(6, (3, 0))
+            quant_h(7, 8)
+            layer2(7, (3, 0))
+            evac(S, 3, 1, 2, 2, 0, 1)
+            evac(V, 0, 1, 2, 2, 1, 2)
+            store(nc.sync, 1, 2, 2, 0, 1)
+            store(nc.sync, 1, 2, 2, 1, 2)

@@ -35,7 +35,7 @@ def tile_rows_gmlp_gelu_kernel(tc, x, w1, hs, w2, out):
         x_bf = tile("x_bf", [P, N * PACK], BF16)
         x_q = tile("x_q", [P, N], U32)
         x_s = tile("x_s", [P, N], U8)
-        w1_raw = [tile("w1_raw%d" % i, [P, 2, K], F32) for i in range(2)]
+        w1_raw = tile("w1_raw", [P, PACK, K], F32)
         w1_bf = tile("w1_bf", [P, K * PACK], BF16)
         w1_q = tile("w1_q", [P, K], U32)
         w1_s = tile("w1_s", [P, K], U8)
@@ -49,7 +49,7 @@ def tile_rows_gmlp_gelu_kernel(tc, x, w1, hs, w2, out):
         h_bf = tile("h_bf", [P, len(STEPS) * CW * PACK], BF16)
         h_q = tile("h_q", [P, len(STEPS) * CW], U32)
         h_s = tile("h_s", [P, len(STEPS) * CW], U8)
-        y_sb = [[tile("y_sb%d_%d" % (g, q), [P, 2, 2 * CW], F32) for q in range(2)] for g in range(G)]
+        y_sb = [tile("y_sb%d" % g, [P, 2, N], F32) for g in range(G)]
         z_ps = [[ps.tile([P, PACK, CW], F32, name="z_ps%d_%d" % (g, b)) for b in range(2)] for g in range(G)]
         y_ps = [ps.tile([P, 2, 2 * CW], F32, name="y_ps%d" % b) for b in range(4)]
 
@@ -66,9 +66,6 @@ def tile_rows_gmlp_gelu_kernel(tc, x, w1, hs, w2, out):
         def load_x(i, q=nc.sync):
             lo, hi = X_PIECES[i]
             q.dma_start(out=x_raw[i][:], in_=x_v[:, :, lo:hi])
-
-        def load_w1(i, q=nc.sync):
-            q.dma_start(out=w1_raw[i][:], in_=w1_v[:, 2 * i:2 * i + 2, :])
 
         def load_w2(g, q=nc.sync):
             q.dma_start(out=w2_raw[g][:], in_=w2[g].rearrange("(p j) m -> p j m", j=PACK))
@@ -88,10 +85,10 @@ def tile_rows_gmlp_gelu_kernel(tc, x, w1, hs, w2, out):
         def cast_w2(eng, g, lo, hi):
             interleave(eng, w2_bf[g][:, PACK * lo:PACK * hi], w2_raw[g][:, :, lo:hi])
 
-        def cast_w1(eng, r0, r1, lo, hi, j0, j1):
+        def cast_w1(eng, r0, r1, lo, hi):
             copy(eng,
-                 w1_bf[:].rearrange("p (r s j) -> p s j r", r=PACK, j=PACK)[:, lo:hi, j0:j1, r0:r1],
-                 w1_raw[j0 // 2][:].rearrange("p j (s r) -> p s j r", r=PACK)[:, lo:hi, :, r0:r1])
+                 w1_bf[:].rearrange("p (r s j) -> p s j r", r=PACK, j=PACK)[:, lo:hi, :, r0:r1],
+                 w1_raw[:].rearrange("p j (s r) -> p s j r", r=PACK)[:, lo:hi, :, r0:r1])
 
         def quant(codes, scales, src, lo, hi):
             V.quantize_mx(out=codes[:, lo:hi].bitcast(FP8X4), scales=scales[:, lo:hi],
@@ -136,6 +133,17 @@ def tile_rows_gmlp_gelu_kernel(tc, x, w1, hs, w2, out):
                 in1=hs_t[:, g0:g1, 0:PACK].unsqueeze(2).to_broadcast([P, g1 - g0, width, PACK]),
                 op=mybir.AluOpType.mult)
 
+        def scale_half(u, half):
+            span = slice((2 * u + half) * CW * 2, (2 * u + half + 1) * CW * 2)
+            V.tensor_tensor(
+                out=h_bf[:, span].rearrange("p (n r) -> p n r", r=PACK),
+                in0=act[:, span].rearrange("p (n r) -> p n r", r=PACK),
+                in1=hs_t[:, STEPS[u][0], 0:PACK].unsqueeze(1).to_broadcast([P, CW // 2, PACK]),
+                op=mybir.AluOpType.mult)
+
+        def quant_half(u, half):
+            quant(h_q, h_s, h_bf, u * CW + half * CW // 2, u * CW + (half + 1) * CW // 2)
+
         def layer2(u, banks):
             g, c = STEPS[u]
             cols = slice(u * CW, (u + 1) * CW)
@@ -149,16 +157,14 @@ def tile_rows_gmlp_gelu_kernel(tc, x, w1, hs, w2, out):
 
         def evac(eng, bank, g, c, chunks=1, t0=0, t1=2):
             lo = (c % 2) * CW
-            copy(eng, y_sb[g][c // 2][:, t0:t1, lo:lo + chunks * CW], y_ps[bank][:, t0:t1, lo:lo + chunks * CW])
+            copy(eng, y_sb[g][:, t0:t1, c * CW:(c + chunks) * CW], y_ps[bank][:, t0:t1, lo:lo + chunks * CW])
 
         def store(q, g, c, chunks=1, t0=0, t1=2):
-            lo = (c % 2) * CW
-            q.dma_start(out=out_v[g][:, t0:t1, c * CW:(c + chunks) * CW],
-                        in_=y_sb[g][c // 2][:, t0:t1, lo:lo + chunks * CW])
+            cols = slice(c * CW, (c + chunks) * CW)
+            q.dma_start(out=out_v[g][:, t0:t1, cols], in_=y_sb[g][:, t0:t1, cols])
 
         with tc.manual_schedule():
-            load_w1(0)
-            load_w1(1)
+            nc.sync.dma_start(out=w1_raw[:], in_=w1_v)
             load_x(0)
             load_x(1)
             load_x(2)
@@ -167,24 +173,22 @@ def tile_rows_gmlp_gelu_kernel(tc, x, w1, hs, w2, out):
             load_hs(nc.scalar)
             nc.gpsimd.memset(warm[:, 0:1], 0.0)
             S.activation(out=warm[:, 1:2], in_=warm[:, 0:1], func=GELU)
-            cast_w1(S, 2, 4, 0, 64, 2, 4)
-            cast_w1(V, 0, 4, 0, 128, 0, 2)
+            cast_w1(S, 2, 4, 0, 80)
+            cast_w1(V, 0, 2, 0, 128)
             cast_x(S, 0, 64)
-            cast_w1(V, 0, 2, 0, 128, 2, 4)
-            cast_x(S, 256, 320)
-            cast_w1(V, 2, 4, 64, 128, 2, 4)
+            cast_w1(V, 2, 4, 80, 128)
+            cast_x(S, 256, 352)
             cast_x(V, 64, 128)
             quant_w1(0, 2)
             quant_x(0, 1)
             layer1(0, 0, 2)
-            layer1(1, 0, 2)
             quant_w1(2, 4)
             layer1(0, 2, 4)
-            layer1(1, 2, 4)
+            layer1(1)
             gelu(0)
             cast_x(V, 128, 256)
             gelu(1)
-            cast_x(V, 320, 384)
+            cast_x(V, 352, 384)
             quant_x(1, 2)
             layer1(2)
             layer1(3)
@@ -193,17 +197,17 @@ def tile_rows_gmlp_gelu_kernel(tc, x, w1, hs, w2, out):
             gelu(3)
             quant_x(2, 3)
             layer1(4)
-            cast_w2(S, 0, 0, 160)
-            scale(0, 1)
-            gelu(4)
+            cast_w2(S, 0, 0, 128)
             quant_x(3, 4)
             layer1(5)
             layer1(6)
             layer1(7)
+            gelu(4)
+            scale(0, 1)
             cast_w2(S, 1, 0, 192)
             scale(1, 2)
             gelu(5)
-            cast_w2(V, 0, 160, 256)
+            cast_w2(V, 0, 128, 256)
             gelu(6)
             scale(2, 3)
             scale(3, 4)

@@ -19,6 +19,7 @@ CW = 128
 RUN = 2
 X_PIECES = [(0, 128), (128, 384), (384, 512)]
 STEPS = [(0, 0), (1, 0), (0, 1), (1, 1), (0, 2), (0, 3), (1, 2), (1, 3)]
+STORES = [(0, 0, 2, 0, 2), (1, 0, 2, 0, 2), (0, 2, 1, 0, 2), (0, 3, 1, 0, 2), (1, 2, 1, 0, 2), (1, 3, 1, 0, 1), (1, 3, 1, 1, 2)]
 
 
 def tile_rows_gmlp_gelu_kernel(tc, x, w1, hs, w2, out):
@@ -49,7 +50,7 @@ def tile_rows_gmlp_gelu_kernel(tc, x, w1, hs, w2, out):
         h_bf = tile("h_bf", [P, len(STEPS) * CW * PACK], BF16)
         h_q = tile("h_q", [P, len(STEPS) * CW], U32)
         h_s = tile("h_s", [P, len(STEPS) * CW], U8)
-        y_sb = [tile("y_sb%d" % g, [P, 2, N], F32) for g in range(G)]
+        y_sb = {s: tile("y_sb%d" % i, [P, s[4] - s[3], s[2] * CW], F32) for i, s in enumerate(STORES)}
         z_ps = [[ps.tile([P, PACK, CW], F32, name="z_ps%d_%d" % (g, b)) for b in range(2)] for g in range(G)]
         y_ps = [ps.tile([P, 2, 2 * CW], F32, name="y_ps%d" % b) for b in range(4)]
 
@@ -157,11 +158,12 @@ def tile_rows_gmlp_gelu_kernel(tc, x, w1, hs, w2, out):
 
         def evac(eng, bank, g, c, chunks=1, t0=0, t1=2):
             lo = (c % 2) * CW
-            copy(eng, y_sb[g][:, t0:t1, c * CW:(c + chunks) * CW], y_ps[bank][:, t0:t1, lo:lo + chunks * CW])
+            s = [s for s in STORES if s[0] == g and s[1] <= c < s[1] + s[2] and s[3] <= t0 < s[4]][0]
+            copy(eng, y_sb[s][:, t0 - s[3]:t1 - s[3], (c - s[1]) * CW:(c - s[1] + chunks) * CW], y_ps[bank][:, t0:t1, lo:lo + chunks * CW])
 
         def store(q, g, c, chunks=1, t0=0, t1=2):
             cols = slice(c * CW, (c + chunks) * CW)
-            q.dma_start(out=out_v[g][:, t0:t1, cols], in_=y_sb[g][:, t0:t1, cols])
+            q.dma_start(out=out_v[g][:, t0:t1, cols], in_=y_sb[(g, c, chunks, t0, t1)][:])
 
         with tc.manual_schedule():
             nc.sync.dma_start(out=w1_raw[:], in_=w1_v)
@@ -197,17 +199,17 @@ def tile_rows_gmlp_gelu_kernel(tc, x, w1, hs, w2, out):
             gelu(3)
             quant_x(2, 3)
             layer1(4)
-            cast_w2(S, 0, 0, 128)
+            cast_w2(S, 0, 0, 160)
+            scale(0, 1)
+            gelu(4)
             quant_x(3, 4)
             layer1(5)
             layer1(6)
             layer1(7)
-            gelu(4)
-            scale(0, 1)
-            cast_w2(S, 1, 0, 192)
+            cast_w2(S, 1, 0, 160)
             scale(1, 2)
             gelu(5)
-            cast_w2(V, 0, 128, 256)
+            cast_w2(V, 0, 160, 256)
             gelu(6)
             scale(2, 3)
             scale(3, 4)
@@ -216,7 +218,7 @@ def tile_rows_gmlp_gelu_kernel(tc, x, w1, hs, w2, out):
             layer2(0, (0, 0))
             layer2(2, (0, 0))
             evac(S, 0, 0, 0, 2)
-            cast_w2(V, 1, 192, 256)
+            cast_w2(V, 1, 160, 256)
             store(nc.sync, 0, 0, 2)
             gelu(7)
             scale(4, 5)
@@ -228,17 +230,23 @@ def tile_rows_gmlp_gelu_kernel(tc, x, w1, hs, w2, out):
             store(nc.sync, 1, 0, 2)
             quant_h(4, 5)
             layer2(4, (2, 2))
+            evac(S, 2, 0, 2, 1)
             scale(6, 7)
+            store(nc.sync, 0, 2, 1)
             quant_h(5, 6)
-            layer2(5, (2, 2))
-            evac(S, 2, 0, 2, 2)
-            scale(7, 8)
-            store(nc.sync, 0, 2, 2)
+            layer2(5, (0, 0))
+            evac(S, 0, 0, 3, 1)
+            scale_half(7, 0)
+            store(nc.sync, 0, 3, 1)
             quant_h(6, 7)
-            layer2(6, (3, 0))
-            quant_h(7, 8)
-            layer2(7, (3, 0))
-            evac(S, 3, 1, 2, 2, 0, 1)
-            evac(V, 0, 1, 2, 2, 1, 2)
-            store(nc.sync, 1, 2, 2, 0, 1)
-            store(nc.sync, 1, 2, 2, 1, 2)
+            layer2(6, (3, 3))
+            evac(S, 3, 1, 2, 1)
+            scale_half(7, 1)
+            store(nc.sync, 1, 2, 1)
+            quant_half(7, 0)
+            quant_half(7, 1)
+            layer2(7, (1, 2))
+            evac(S, 1, 1, 3, 1, 0, 1)
+            evac(V, 2, 1, 3, 1, 1, 2)
+            store(nc.sync, 1, 3, 1, 0, 1)
+            store(nc.sync, 1, 3, 1, 1, 2)

@@ -36,7 +36,7 @@ def tile_rows_gmlp_gelu_kernel(tc, x, w1, hs, w2, out):
         x_bf = tile("x_bf", [P, N * PACK], BF16)
         x_q = tile("x_q", [P, N], U32)
         x_s = tile("x_s", [P, N], U8)
-        w1_raw = tile("w1_raw", [P, PACK, K], F32)
+        w1_raw = [tile("w1_raw%d" % i, [P, 2, K], F32) for i in range(2)]
         w1_bf = tile("w1_bf", [P, K * PACK], BF16)
         w1_q = tile("w1_q", [P, K], U32)
         w1_s = tile("w1_s", [P, K], U8)
@@ -68,6 +68,9 @@ def tile_rows_gmlp_gelu_kernel(tc, x, w1, hs, w2, out):
             lo, hi = X_PIECES[i]
             q.dma_start(out=x_raw[i][:], in_=x_v[:, :, lo:hi])
 
+        def load_w1(i, q=nc.sync):
+            q.dma_start(out=w1_raw[i][:], in_=w1_v[:, 2 * i:2 * i + 2, :])
+
         def load_w2(g, q=nc.sync):
             q.dma_start(out=w2_raw[g][:], in_=w2[g].rearrange("(p j) m -> p j m", j=PACK))
 
@@ -86,10 +89,10 @@ def tile_rows_gmlp_gelu_kernel(tc, x, w1, hs, w2, out):
         def cast_w2(eng, g, lo, hi):
             interleave(eng, w2_bf[g][:, PACK * lo:PACK * hi], w2_raw[g][:, :, lo:hi])
 
-        def cast_w1(eng, r0, r1, lo, hi):
+        def cast_w1(eng, r0, r1, lo, hi, j0, j1):
             copy(eng,
-                 w1_bf[:].rearrange("p (r s j) -> p s j r", r=PACK, j=PACK)[:, lo:hi, :, r0:r1],
-                 w1_raw[:].rearrange("p j (s r) -> p s j r", r=PACK)[:, lo:hi, :, r0:r1])
+                 w1_bf[:].rearrange("p (r s j) -> p s j r", r=PACK, j=PACK)[:, lo:hi, j0:j1, r0:r1],
+                 w1_raw[j0 // 2][:].rearrange("p j (s r) -> p s j r", r=PACK)[:, lo:hi, :, r0:r1])
 
         def quant(codes, scales, src, lo, hi):
             V.quantize_mx(out=codes[:, lo:hi].bitcast(FP8X4), scales=scales[:, lo:hi],
@@ -166,7 +169,8 @@ def tile_rows_gmlp_gelu_kernel(tc, x, w1, hs, w2, out):
             q.dma_start(out=out_v[g][:, t0:t1, cols], in_=y_sb[(g, c, chunks, t0, t1)][:])
 
         with tc.manual_schedule():
-            nc.sync.dma_start(out=w1_raw[:], in_=w1_v)
+            load_w1(0)
+            load_w1(1)
             load_x(0)
             load_x(1)
             load_x(2)
@@ -175,11 +179,12 @@ def tile_rows_gmlp_gelu_kernel(tc, x, w1, hs, w2, out):
             load_hs(nc.scalar)
             nc.gpsimd.memset(warm[:, 0:1], 0.0)
             S.activation(out=warm[:, 1:2], in_=warm[:, 0:1], func=GELU)
-            cast_w1(S, 2, 4, 0, 80)
-            cast_w1(V, 0, 2, 0, 128)
+            cast_w1(S, 2, 4, 0, 64, 2, 4)
+            cast_w1(V, 0, 4, 0, 128, 0, 2)
             cast_x(S, 0, 64)
-            cast_w1(V, 2, 4, 80, 128)
+            cast_w1(V, 0, 2, 0, 128, 2, 4)
             cast_x(S, 256, 352)
+            cast_w1(V, 2, 4, 64, 128, 2, 4)
             cast_x(V, 64, 128)
             quant_w1(0, 2)
             quant_x(0, 1)

@@ -127,6 +127,13 @@ def tile_rows_gmlp_gelu_kernel(tc, x, w1, hs, w2, out):
             S.activation(out=act[:, u * CW * PACK:(u + 1) * CW * PACK].rearrange("p (n r) -> p n r", r=PACK),
                          in_=z_ps[g][c % 2][:].rearrange("p r n -> p n r"), func=GELU)
 
+        def gelu_half(u, half):
+            g, c = STEPS[u]
+            span = slice((2 * u + half) * CW * 2, (2 * u + half + 1) * CW * 2)
+            cols = slice(half * CW // 2, (half + 1) * CW // 2)
+            S.activation(out=act[:, span].rearrange("p (n r) -> p n r", r=PACK),
+                         in_=z_ps[g][c % 2][:, :, cols].rearrange("p r n -> p n r"), func=GELU)
+
         def scale(u0, u1):
             g0, g1 = STEPS[u0][0], STEPS[u1 - 1][0] + 1
             span = slice(u0 * CW * PACK, u1 * CW * PACK)
@@ -179,12 +186,12 @@ def tile_rows_gmlp_gelu_kernel(tc, x, w1, hs, w2, out):
             load_hs(nc.scalar)
             nc.gpsimd.memset(warm[:, 0:1], 0.0)
             S.activation(out=warm[:, 1:2], in_=warm[:, 0:1], func=GELU)
-            cast_w1(S, 2, 4, 0, 64, 2, 4)
+            cast_w1(S, 2, 4, 0, 80, 2, 4)
             cast_w1(V, 0, 4, 0, 128, 0, 2)
             cast_x(S, 0, 64)
             cast_w1(V, 0, 2, 0, 128, 2, 4)
-            cast_x(S, 256, 352)
-            cast_w1(V, 2, 4, 64, 128, 2, 4)
+            cast_x(S, 128, 192)
+            cast_w1(V, 2, 4, 80, 128, 2, 4)
             cast_x(V, 64, 128)
             quant_w1(0, 2)
             quant_x(0, 1)
@@ -192,10 +199,11 @@ def tile_rows_gmlp_gelu_kernel(tc, x, w1, hs, w2, out):
             quant_w1(2, 4)
             layer1(0, 2, 4)
             layer1(1)
-            gelu(0)
-            cast_x(V, 128, 256)
+            gelu_half(0, 0)
+            cast_x(V, 192, 256)
+            gelu_half(0, 1)
+            cast_x(V, 256, 384)
             gelu(1)
-            cast_x(V, 352, 384)
             quant_x(1, 2)
             layer1(2)
             layer1(3)
@@ -204,23 +212,25 @@ def tile_rows_gmlp_gelu_kernel(tc, x, w1, hs, w2, out):
             gelu(3)
             quant_x(2, 3)
             layer1(4)
-            cast_w2(S, 0, 0, 160)
-            scale(0, 1)
+            cast_w2(S, 0, 0, 128)
+            scale_half(0, 0)
             gelu(4)
+            scale_half(0, 1)
+            cast_w2(S, 1, 0, 160)
             quant_x(3, 4)
             layer1(5)
             layer1(6)
             layer1(7)
-            cast_w2(S, 1, 0, 160)
-            scale(1, 2)
             gelu(5)
-            cast_w2(V, 0, 160, 256)
+            scale(1, 2)
             gelu(6)
+            cast_w2(V, 0, 128, 256)
             scale(2, 3)
             scale(3, 4)
+            quant_h(0, 2)
             quant_w2(0)
-            quant_h(0, 4)
             layer2(0, (0, 0))
+            quant_h(2, 4)
             layer2(2, (0, 0))
             evac(S, 0, 0, 0, 2)
             cast_w2(V, 1, 160, 256)

@@ -62,7 +62,7 @@ def tile_rows_gmlp_gelu_kernel(tc, x, w1, hs, w2, out):
             if eng is S:
                 S.copy(out=dst, in_=src)
             else:
-                V.tensor_copy(out=dst, in_=src)
+                eng.tensor_copy(out=dst, in_=src)
 
         def load_x(i, q=nc.sync):
             lo, hi = X_PIECES[i]
@@ -74,7 +74,7 @@ def tile_rows_gmlp_gelu_kernel(tc, x, w1, hs, w2, out):
         def load_w2(g, q=nc.sync):
             q.dma_start(out=w2_raw[g][:], in_=w2[g].rearrange("(p j) m -> p j m", j=PACK))
 
-        def load_hs(q):
+        def load_hs(q=nc.sync):
             q.dma_start(out=hs_t[:, :, 0:PACK], in_=hs.rearrange("g (p r) o -> p g (r o)", r=PACK))
 
         def interleave(eng, dst, src):
@@ -89,10 +89,10 @@ def tile_rows_gmlp_gelu_kernel(tc, x, w1, hs, w2, out):
         def cast_w2(eng, g, lo, hi):
             interleave(eng, w2_bf[g][:, PACK * lo:PACK * hi], w2_raw[g][:, :, lo:hi])
 
-        def cast_w1(eng, r0, r1, lo, hi, j0, j1):
+        def cast_w1(eng, half, r0, r1, lo=0, hi=P):
             copy(eng,
-                 w1_bf[:].rearrange("p (r s j) -> p s j r", r=PACK, j=PACK)[:, lo:hi, j0:j1, r0:r1],
-                 w1_raw[j0 // 2][:].rearrange("p j (s r) -> p s j r", r=PACK)[:, lo:hi, :, r0:r1])
+                 w1_bf[:].rearrange("p (r s j) -> p s j r", r=PACK, j=PACK)[:, lo:hi, 2 * half:2 * half + 2, r0:r1],
+                 w1_raw[half][:].rearrange("p j (s r) -> p s j r", r=PACK)[:, lo:hi, :, r0:r1])
 
         def quant(codes, scales, src, lo, hi):
             V.quantize_mx(out=codes[:, lo:hi].bitcast(FP8X4), scales=scales[:, lo:hi],
@@ -104,64 +104,63 @@ def tile_rows_gmlp_gelu_kernel(tc, x, w1, hs, w2, out):
         def quant_x(c0, c1):
             quant(x_q, x_s, x_bf, c0 * CW, c1 * CW)
 
-        def quant_w2(g):
-            quant(w2_q[g], w2_s[g], w2_bf[g], 0, M)
+        def quant_w2(g, lo=0, hi=M):
+            quant(w2_q[g], w2_s[g], w2_bf[g], lo, hi)
 
-        def quant_h(u0, u1):
-            quant(h_q, h_s, h_bf, u0 * CW, u1 * CW)
+        def quant_h(u, lo=0, hi=CW):
+            quant(h_q, h_s, h_bf, u * CW + lo, u * CW + hi)
 
-        def layer1(u, r0=0, r1=PACK):
+        def product(u, r, dst):
             g, c = STEPS[u]
             rows = slice(ROWS * g, ROWS * (g + 1))
             cols = slice(c * CW, (c + 1) * CW)
-            for r in range(r0, r1):
-                ks = slice(r * P, (r + 1) * P)
-                nc.tensor.matmul_mx(
-                    out=z_ps[g][c % 2][:, r, :],
-                    lhsT=w1_q[rows, ks].bitcast(FP8X4), lhsT_scale=w1_s[rows, ks],
-                    rhs=x_q[rows, cols].bitcast(FP8X4), rhs_scale=x_s[rows, cols],
-                    start=True, stop=True)
+            ks = slice(r * P, (r + 1) * P)
+            nc.tensor.matmul_mx(
+                out=dst,
+                lhsT=w1_q[rows, ks].bitcast(FP8X4), lhsT_scale=w1_s[rows, ks],
+                rhs=x_q[rows, cols].bitcast(FP8X4), rhs_scale=x_s[rows, cols],
+                start=True, stop=True)
 
-        def gelu(u):
-            g, c = STEPS[u]
-            S.activation(out=act[:, u * CW * PACK:(u + 1) * CW * PACK].rearrange("p (n r) -> p n r", r=PACK),
-                         in_=z_ps[g][c % 2][:].rearrange("p r n -> p n r"), func=GELU)
+        def layer1(u, bank):
+            for r in range(PACK):
+                product(u, r, z_ps[STEPS[u][0]][bank][:, r, :])
 
-        def gelu_half(u, half):
-            g, c = STEPS[u]
-            span = slice((2 * u + half) * CW * 2, (2 * u + half + 1) * CW * 2)
-            cols = slice(half * CW // 2, (half + 1) * CW // 2)
-            S.activation(out=act[:, span].rearrange("p (n r) -> p n r", r=PACK),
-                         in_=z_ps[g][c % 2][:, :, cols].rearrange("p r n -> p n r"), func=GELU)
+        def layer1_pair(u, pair):
+            for e in range(2):
+                product(u, 2 * pair + e, z_ps[STEPS[u][0]][pair][:, e, :])
 
-        def scale(u0, u1):
-            g0, g1 = STEPS[u0][0], STEPS[u1 - 1][0] + 1
-            span = slice(u0 * CW * PACK, u1 * CW * PACK)
-            width = (u1 - u0) * CW // (g1 - g0)
+        def step_of(t, u):
+            return t[:, u * CW * PACK:(u + 1) * CW * PACK]
+
+        def gelu(u, bank, lo=0, hi=CW):
+            S.activation(out=step_of(act, u).rearrange("p (n r) -> p n r", r=PACK)[:, lo:hi, :],
+                         in_=z_ps[STEPS[u][0]][bank][:].rearrange("p r n -> p n r")[:, lo:hi, :], func=GELU)
+
+        def gelu_pair(u, pair):
+            S.activation(out=step_of(act, u).rearrange("p (h n e) -> p h n e", h=2, e=2)[:, pair, :, :],
+                         in_=z_ps[STEPS[u][0]][pair][:, 0:2, :].rearrange("p e n -> p n e"), func=GELU)
+
+        def scale(u, lo=0, hi=CW):
             V.tensor_tensor(
-                out=h_bf[:, span].rearrange("p (g n r) -> p g n r", g=g1 - g0, r=PACK),
-                in0=act[:, span].rearrange("p (g n r) -> p g n r", g=g1 - g0, r=PACK),
-                in1=hs_t[:, g0:g1, 0:PACK].unsqueeze(2).to_broadcast([P, g1 - g0, width, PACK]),
+                out=step_of(h_bf, u).rearrange("p (n r) -> p n r", r=PACK)[:, lo:hi, :],
+                in0=step_of(act, u).rearrange("p (n r) -> p n r", r=PACK)[:, lo:hi, :],
+                in1=hs_t[:, STEPS[u][0], 0:PACK].unsqueeze(1).to_broadcast([P, hi - lo, PACK]),
                 op=mybir.AluOpType.mult)
 
-        def scale_half(u, half):
-            span = slice((2 * u + half) * CW * 2, (2 * u + half + 1) * CW * 2)
+        def scale_pairs(u, lo=0, hi=CW):
             V.tensor_tensor(
-                out=h_bf[:, span].rearrange("p (n r) -> p n r", r=PACK),
-                in0=act[:, span].rearrange("p (n r) -> p n r", r=PACK),
-                in1=hs_t[:, STEPS[u][0], 0:PACK].unsqueeze(1).to_broadcast([P, CW // 2, PACK]),
+                out=step_of(h_bf, u).rearrange("p (n h e) -> p n h e", h=2, e=2)[:, lo:hi, :, :],
+                in0=step_of(act, u).rearrange("p (h n e) -> p n h e", h=2, e=2)[:, lo:hi, :, :],
+                in1=hs_t[:, STEPS[u][0], 0:PACK].rearrange("p (h e) -> p h e", h=2).unsqueeze(1).to_broadcast([P, hi - lo, 2, 2]),
                 op=mybir.AluOpType.mult)
 
-        def quant_half(u, half):
-            quant(h_q, h_s, h_bf, u * CW + half * CW // 2, u * CW + (half + 1) * CW // 2)
-
-        def layer2(u, banks):
+        def layer2(u, bank0, bank1=None):
             g, c = STEPS[u]
             cols = slice(u * CW, (u + 1) * CW)
-            for t in range(2):
+            for t, bank in enumerate((bank0, bank0 if bank1 is None else bank1)):
                 ms = slice(t * P, (t + 1) * P)
                 nc.tensor.matmul_mx(
-                    out=y_ps[banks[t]][:, t, (c % 2) * CW:(c % 2 + 1) * CW],
+                    out=y_ps[bank][:, t, (c % 2) * CW:(c % 2 + 1) * CW],
                     lhsT=w2_q[g][:, ms].bitcast(FP8X4), lhsT_scale=w2_s[g][:, ms],
                     rhs=h_q[:, cols].bitcast(FP8X4), rhs_scale=h_s[:, cols],
                     start=True, stop=True)
@@ -171,97 +170,102 @@ def tile_rows_gmlp_gelu_kernel(tc, x, w1, hs, w2, out):
             s = [s for s in STORES if s[0] == g and s[1] <= c < s[1] + s[2] and s[3] <= t0 < s[4]][0]
             copy(eng, y_sb[s][:, t0 - s[3]:t1 - s[3], (c - s[1]) * CW:(c - s[1] + chunks) * CW], y_ps[bank][:, t0:t1, lo:lo + chunks * CW])
 
-        def store(q, g, c, chunks=1, t0=0, t1=2):
-            cols = slice(c * CW, (c + chunks) * CW)
-            q.dma_start(out=out_v[g][:, t0:t1, cols], in_=y_sb[(g, c, chunks, t0, t1)][:])
+        def store(i, q=nc.sync):
+            g, c, chunks, t0, t1 = STORES[i]
+            q.dma_start(out=out_v[g][:, t0:t1, c * CW:(c + chunks) * CW], in_=y_sb[STORES[i]][:])
 
         with tc.manual_schedule():
             load_w1(0)
             load_w1(1)
             load_x(0)
             load_x(1)
+            load_hs()
             load_x(2)
             load_w2(0)
             load_w2(1)
-            load_hs(nc.scalar)
-            nc.gpsimd.memset(warm[:, 0:1], 0.0)
+            V.memset(warm[:, 0:1], 0.0)
             S.activation(out=warm[:, 1:2], in_=warm[:, 0:1], func=GELU)
-            cast_w1(S, 2, 4, 0, 80, 2, 4)
-            cast_w1(V, 0, 4, 0, 128, 0, 2)
-            cast_x(S, 0, 64)
-            cast_w1(V, 0, 2, 0, 128, 2, 4)
-            cast_x(S, 128, 192)
-            cast_w1(V, 2, 4, 80, 128, 2, 4)
-            cast_x(V, 64, 128)
+            cast_w1(V, 0, 0, 4)
+            cast_w1(V, 1, 0, 2)
+            cast_w1(S, 1, 2, 4, 0, 80)
+            cast_w1(V, 1, 2, 4, 80, 128)
+            cast_x(S, 0, 48)
+            cast_x(V, 48, 128)
             quant_w1(0, 2)
             quant_x(0, 1)
-            layer1(0, 0, 2)
+            layer1_pair(0, 0)
             quant_w1(2, 4)
-            layer1(0, 2, 4)
-            layer1(1)
-            gelu_half(0, 0)
-            cast_x(V, 192, 256)
-            gelu_half(0, 1)
-            cast_x(V, 256, 384)
-            gelu(1)
+            layer1_pair(0, 1)
+            layer1_pair(1, 0)
+            layer1_pair(1, 1)
+            cast_x(V, 128, 256)
+            cast_x(S, 256, 320)
+            cast_x(V, 320, 384)
             quant_x(1, 2)
-            layer1(2)
-            layer1(3)
-            gelu(2)
-            cast_x(V, 384, 512)
-            gelu(3)
+            gelu_pair(0, 0)
+            gelu_pair(0, 1)
+            layer1_pair(2, 0)
+            layer1_pair(2, 1)
+            gelu_pair(1, 0)
+            gelu_pair(1, 1)
+            layer1_pair(3, 0)
+            layer1_pair(3, 1)
             quant_x(2, 3)
-            layer1(4)
-            cast_w2(S, 0, 0, 128)
-            scale_half(0, 0)
-            gelu(4)
-            scale_half(0, 1)
-            cast_w2(S, 1, 0, 160)
+            cast_x(V, 384, 512)
+            scale_pairs(0)
             quant_x(3, 4)
-            layer1(5)
-            layer1(6)
-            layer1(7)
-            gelu(5)
-            scale(1, 2)
-            gelu(6)
-            cast_w2(V, 0, 128, 256)
-            scale(2, 3)
-            scale(3, 4)
-            quant_h(0, 2)
+            gelu_pair(2, 0)
+            layer1(4, 0)
+            gelu_pair(2, 1)
+            layer1(5, 1)
+            scale_pairs(1)
+            gelu_pair(3, 0)
+            layer1(6, 0)
+            gelu_pair(3, 1)
+            layer1(7, 1)
+            cast_w2(V, 0, 112, 256)
+            cast_w2(S, 0, 0, 112)
+            scale_pairs(2)
+            gelu(4, 0)
+            quant_h(0, 0, 256)
+            scale_pairs(3)
             quant_w2(0)
-            layer2(0, (0, 0))
-            quant_h(2, 4)
-            layer2(2, (0, 0))
-            evac(S, 0, 0, 0, 2)
+            layer2(0, 0)
+            gelu(5, 1)
+            quant_h(2, 0, 256)
+            layer2(2, 0)
+            cast_w2(S, 1, 0, 160)
             cast_w2(V, 1, 160, 256)
-            store(nc.sync, 0, 0, 2)
-            gelu(7)
-            scale(4, 5)
+            scale(4)
+            gelu(6, 0)
+            evac(S, 0, 0, 0, 2)
+            store(0)
             quant_w2(1)
-            layer2(1, (1, 1))
-            layer2(3, (1, 1))
+            layer2(1, 1)
+            layer2(3, 1)
+            scale(5)
+            gelu(7, 1)
+            quant_h(4)
+            layer2(4, 2)
             evac(S, 1, 1, 0, 2)
-            scale(5, 6)
-            store(nc.sync, 1, 0, 2)
-            quant_h(4, 5)
-            layer2(4, (2, 2))
-            evac(S, 2, 0, 2, 1)
-            scale(6, 7)
-            store(nc.sync, 0, 2, 1)
-            quant_h(5, 6)
-            layer2(5, (0, 0))
-            evac(S, 0, 0, 3, 1)
-            scale_half(7, 0)
-            store(nc.sync, 0, 3, 1)
-            quant_h(6, 7)
-            layer2(6, (3, 3))
-            evac(S, 3, 1, 2, 1)
-            scale_half(7, 1)
-            store(nc.sync, 1, 2, 1)
-            quant_half(7, 0)
-            quant_half(7, 1)
-            layer2(7, (1, 2))
+            store(1)
+            scale(6)
+            quant_h(5)
+            layer2(5, 3)
+            evac(S, 2, 0, 2)
+            store(2)
+            evac(S, 3, 0, 3)
+            store(3)
+            scale(7, 0, 64)
+            quant_h(6)
+            layer2(6, 0)
+            evac(S, 0, 1, 2)
+            store(4)
+            scale(7, 64, 128)
+            quant_h(7, 0, 64)
+            quant_h(7, 64, 128)
+            layer2(7, 1, 2)
             evac(S, 1, 1, 3, 1, 0, 1)
             evac(V, 2, 1, 3, 1, 1, 2)
-            store(nc.sync, 1, 3, 1, 0, 1)
-            store(nc.sync, 1, 3, 1, 1, 2)
+            store(5)
+            store(6)

@@ -20,6 +20,9 @@ RUN = 2
 X_PIECES = [(0, 128), (128, 384), (384, 512)]
 STEPS = [(0, 0), (1, 0), (0, 1), (1, 1), (0, 2), (0, 3), (1, 2), (1, 3)]
 STORES = [(0, 0, 2, 0, 2), (1, 0, 2, 0, 2), (0, 2, 1, 0, 2), (0, 3, 1, 0, 2), (1, 2, 1, 0, 2), (1, 3, 1, 0, 1), (1, 3, 1, 1, 2)]
+W2_AT = [0, 768]
+H_AT = [256, 512, 384, 640, 1024, 1152, 1280, 1408]
+L2_WORDS = G * M + len(STEPS) * CW
 
 
 def tile_rows_gmlp_gelu_kernel(tc, x, w1, hs, w2, out):
@@ -41,15 +44,12 @@ def tile_rows_gmlp_gelu_kernel(tc, x, w1, hs, w2, out):
         w1_q = tile("w1_q", [P, K], U32)
         w1_s = tile("w1_s", [P, K], U8)
         w2_raw = [tile("w2_raw%d" % g, [P, PACK, M], F32) for g in range(G)]
-        w2_bf = [tile("w2_bf%d" % g, [P, M * PACK], BF16) for g in range(G)]
-        w2_q = [tile("w2_q%d" % g, [P, M], U32) for g in range(G)]
-        w2_s = [tile("w2_s%d" % g, [P, M], U8) for g in range(G)]
         hs_t = tile("hs_t", [P, G, 8], F32)
         warm = tile("warm", [P, 2], F32)
         act = tile("act", [P, len(STEPS) * CW * PACK], F32)
-        h_bf = tile("h_bf", [P, len(STEPS) * CW * PACK], BF16)
-        h_q = tile("h_q", [P, len(STEPS) * CW], U32)
-        h_s = tile("h_s", [P, len(STEPS) * CW], U8)
+        l2_bf = tile("l2_bf", [P, L2_WORDS * PACK], BF16)
+        l2_q = tile("l2_q", [P, L2_WORDS], U32)
+        l2_s = tile("l2_s", [P, L2_WORDS], U8)
         y_sb = {s: tile("y_sb%d" % i, [P, s[4] - s[3], s[2] * CW], F32) for i, s in enumerate(STORES)}
         z_ps = [[ps.tile([P, PACK, CW], F32, name="z_ps%d_%d" % (g, b)) for b in range(2)] for g in range(G)]
         y_ps = [ps.tile([P, 2, 2 * CW], F32, name="y_ps%d" % b) for b in range(4)]
@@ -87,7 +87,7 @@ def tile_rows_gmlp_gelu_kernel(tc, x, w1, hs, w2, out):
             interleave(eng, x_bf[:, PACK * lo:PACK * hi], x_raw[i][:, :, lo - first:hi - first])
 
         def cast_w2(eng, g, lo, hi):
-            interleave(eng, w2_bf[g][:, PACK * lo:PACK * hi], w2_raw[g][:, :, lo:hi])
+            interleave(eng, l2_bf[:, PACK * (W2_AT[g] + lo):PACK * (W2_AT[g] + hi)], w2_raw[g][:, :, lo:hi])
 
         def cast_w1(eng, half, r0, r1, lo=0, hi=P):
             copy(eng,
@@ -104,11 +104,17 @@ def tile_rows_gmlp_gelu_kernel(tc, x, w1, hs, w2, out):
         def quant_x(c0, c1):
             quant(x_q, x_s, x_bf, c0 * CW, c1 * CW)
 
-        def quant_w2(g, lo=0, hi=M):
-            quant(w2_q[g], w2_s[g], w2_bf[g], lo, hi)
+        def quant_l2(lo, hi):
+            quant(l2_q, l2_s, l2_bf, lo, hi)
 
         def quant_h(u, lo=0, hi=CW):
-            quant(h_q, h_s, h_bf, u * CW + lo, u * CW + hi)
+            quant_l2(H_AT[u] + lo, H_AT[u] + hi)
+
+        def quant_w2(g):
+            quant_l2(W2_AT[g], W2_AT[g] + M)
+
+        def h_of(u, steps=1):
+            return l2_bf[:, PACK * H_AT[u]:PACK * (H_AT[u] + steps * CW)]
 
         def product(u, r, dst):
             g, c = STEPS[u]
@@ -142,27 +148,34 @@ def tile_rows_gmlp_gelu_kernel(tc, x, w1, hs, w2, out):
 
         def scale(u, lo=0, hi=CW):
             V.tensor_tensor(
-                out=step_of(h_bf, u).rearrange("p (n r) -> p n r", r=PACK)[:, lo:hi, :],
+                out=h_of(u).rearrange("p (n r) -> p n r", r=PACK)[:, lo:hi, :],
                 in0=step_of(act, u).rearrange("p (n r) -> p n r", r=PACK)[:, lo:hi, :],
                 in1=hs_t[:, STEPS[u][0], 0:PACK].unsqueeze(1).to_broadcast([P, hi - lo, PACK]),
                 op=mybir.AluOpType.mult)
 
+        def scale_two(u):
+            V.tensor_tensor(
+                out=h_of(u, 2).rearrange("p (n r) -> p n r", r=PACK),
+                in0=act[:, u * CW * PACK:(u + 2) * CW * PACK].rearrange("p (n r) -> p n r", r=PACK),
+                in1=hs_t[:, STEPS[u][0], 0:PACK].unsqueeze(1).to_broadcast([P, 2 * CW, PACK]),
+                op=mybir.AluOpType.mult)
+
         def scale_pairs(u, lo=0, hi=CW):
             V.tensor_tensor(
-                out=step_of(h_bf, u).rearrange("p (n h e) -> p n h e", h=2, e=2)[:, lo:hi, :, :],
+                out=h_of(u).rearrange("p (n h e) -> p n h e", h=2, e=2)[:, lo:hi, :, :],
                 in0=step_of(act, u).rearrange("p (h n e) -> p n h e", h=2, e=2)[:, lo:hi, :, :],
                 in1=hs_t[:, STEPS[u][0], 0:PACK].rearrange("p (h e) -> p h e", h=2).unsqueeze(1).to_broadcast([P, hi - lo, 2, 2]),
                 op=mybir.AluOpType.mult)
 
         def layer2(u, bank0, bank1=None):
             g, c = STEPS[u]
-            cols = slice(u * CW, (u + 1) * CW)
+            cols = slice(H_AT[u], H_AT[u] + CW)
             for t, bank in enumerate((bank0, bank0 if bank1 is None else bank1)):
-                ms = slice(t * P, (t + 1) * P)
+                ms = slice(W2_AT[g] + t * P, W2_AT[g] + (t + 1) * P)
                 nc.tensor.matmul_mx(
                     out=y_ps[bank][:, t, (c % 2) * CW:(c % 2 + 1) * CW],
-                    lhsT=w2_q[g][:, ms].bitcast(FP8X4), lhsT_scale=w2_s[g][:, ms],
-                    rhs=h_q[:, cols].bitcast(FP8X4), rhs_scale=h_s[:, cols],
+                    lhsT=l2_q[:, ms].bitcast(FP8X4), lhsT_scale=l2_s[:, ms],
+                    rhs=l2_q[:, cols].bitcast(FP8X4), rhs_scale=l2_s[:, cols],
                     start=True, stop=True)
 
         def evac(eng, bank, g, c, chunks=1, t0=0, t1=2):
@@ -196,72 +209,62 @@ def tile_rows_gmlp_gelu_kernel(tc, x, w1, hs, w2, out):
             layer1_pair(0, 0)
             quant_w1(2, 4)
             layer1_pair(0, 1)
-            layer1_pair(1, 0)
-            layer1_pair(1, 1)
+            layer1(1, 0)
             cast_x(V, 128, 256)
             cast_x(S, 256, 320)
             cast_x(V, 320, 384)
             quant_x(1, 2)
             gelu_pair(0, 0)
+            layer1(2, 0)
+            layer1(3, 1)
             gelu_pair(0, 1)
-            layer1_pair(2, 0)
-            layer1_pair(2, 1)
-            gelu_pair(1, 0)
-            gelu_pair(1, 1)
-            layer1_pair(3, 0)
-            layer1_pair(3, 1)
             quant_x(2, 3)
+            layer1(4, 1)
+            gelu(1, 0)
             cast_x(V, 384, 512)
             scale_pairs(0)
             quant_x(3, 4)
-            gelu_pair(2, 0)
-            layer1(4, 0)
-            gelu_pair(2, 1)
-            layer1(5, 1)
-            scale_pairs(1)
-            gelu_pair(3, 0)
+            scale(1)
+            gelu(2, 0)
+            layer1(5, 0)
             layer1(6, 0)
-            gelu_pair(3, 1)
+            gelu(3, 1)
             layer1(7, 1)
-            cast_w2(V, 0, 112, 256)
-            cast_w2(S, 0, 0, 112)
-            scale_pairs(2)
-            gelu(4, 0)
-            quant_h(0, 0, 256)
-            scale_pairs(3)
-            quant_w2(0)
+            cast_w2(V, 0, 0, 256)
+            cast_w2(S, 1, 0, 256)
+            scale(2)
+            scale(3)
+            gelu(4, 1)
+            quant_l2(0, 512)
             layer2(0, 0)
-            gelu(5, 1)
-            quant_h(2, 0, 256)
             layer2(2, 0)
-            cast_w2(S, 1, 0, 160)
-            cast_w2(V, 1, 160, 256)
-            scale(4)
-            gelu(6, 0)
-            evac(S, 0, 0, 0, 2)
-            store(0)
-            quant_w2(1)
+            gelu(5, 0)
+            quant_l2(512, 1024)
             layer2(1, 1)
             layer2(3, 1)
-            scale(5)
+            gelu(6, 0)
+            scale(4)
             gelu(7, 1)
+            scale(5)
+            evac(S, 0, 0, 0, 2)
+            store(0)
             quant_h(4)
             layer2(4, 2)
+            scale(6)
             evac(S, 1, 1, 0, 2)
             store(1)
-            scale(6)
             quant_h(5)
             layer2(5, 3)
             evac(S, 2, 0, 2)
             store(2)
-            evac(S, 3, 0, 3)
-            store(3)
             scale(7, 0, 64)
             quant_h(6)
             layer2(6, 0)
+            evac(S, 3, 0, 3)
+            store(3)
+            scale(7, 64, 128)
             evac(S, 0, 1, 2)
             store(4)
-            scale(7, 64, 128)
             quant_h(7, 0, 64)
             quant_h(7, 64, 128)
             layer2(7, 1, 2)

@@ -16,7 +16,7 @@ P = 128
 PACK = 4
 ROWS = D // PACK
 CW = 128
-RUN = 2
+RUN = 4
 X_PIECES = [(0, 128), (128, 384), (384, 512)]
 STEPS = [(0, 0), (1, 0), (0, 1), (1, 1), (0, 2), (0, 3), (1, 2), (1, 3)]
 STORES = [(0, 0, 2, 0, 2), (1, 0, 2, 0, 2), (0, 2, 1, 0, 2), (0, 3, 1, 0, 2), (1, 2, 1, 0, 2), (1, 3, 1, 0, 1), (1, 3, 1, 1, 2)]

@@ -244,15 +244,15 @@ def tile_rows_gmlp_gelu_kernel(tc, x, w1, hs, w2, out):
             layer2(3, 1)
             gelu(6, 0)
             scale(4)
-            gelu(7, 1)
-            scale(5)
             evac(S, 0, 0, 0, 2)
             store(0)
+            gelu(7, 1)
+            scale(5)
+            evac(S, 1, 1, 0, 2)
+            store(1)
             quant_h(4)
             layer2(4, 2)
             scale(6)
-            evac(S, 1, 1, 0, 2)
-            store(1)
             quant_h(5)
             layer2(5, 3)
             evac(S, 2, 0, 2)

@@ -33,7 +33,7 @@ def tile_rows_gmlp_gelu_kernel(tc, x, w1, hs, w2, out):
         ps = ctx.enter_context(tc.psum_pool(name="ps", bufs=1))
 
         def tile(name, shape, dtype):
-            return sb.tile(shape, dtype, name=name, align_bytes=64)
+            return sb.tile(shape, dtype, name=name, align_bytes=256)
 
         x_raw = [tile("x_raw%d" % i, [P, PACK, hi - lo], F32) for i, (lo, hi) in enumerate(X_PIECES)]
         x_bf = tile("x_bf", [P, N * PACK], BF16)

@@ -17,11 +17,11 @@ PACK = 4
 ROWS = D // PACK
 CW = 128
 RUN = 4
-X_PIECES = [(0, 128), (128, 384), (384, 512)]
-STEPS = [(0, 0), (1, 0), (0, 1), (1, 1), (0, 2), (0, 3), (1, 2), (1, 3)]
-STORES = [(0, 0, 2, 0, 2), (1, 0, 2, 0, 2), (0, 2, 1, 0, 2), (0, 3, 1, 0, 2), (1, 2, 1, 0, 2), (1, 3, 1, 0, 1), (1, 3, 1, 1, 2)]
-W2_AT = [0, 768]
-H_AT = [256, 512, 384, 640, 1024, 1152, 1280, 1408]
+X_PIECES = [(0, 128), (128, 256), (256, 512)]
+STEPS = [(0, 0), (1, 0), (1, 1), (0, 1), (1, 2), (1, 3), (0, 2), (0, 3)]
+STORES = [(1, 0, 2, 0, 2), (0, 0, 2, 0, 2), (1, 2, 1, 0, 2), (1, 3, 1, 0, 2), (0, 2, 1, 0, 2), (0, 3, 1, 0, 1), (0, 3, 1, 1, 2)]
+W2_AT = [768, 0]
+H_AT = [512, 256, 384, 640, 1024, 1152, 1280, 1408]
 L2_WORDS = G * M + len(STEPS) * CW
 
 
@@ -131,6 +131,10 @@ def tile_rows_gmlp_gelu_kernel(tc, x, w1, hs, w2, out):
             for r in range(PACK):
                 product(u, r, z_ps[STEPS[u][0]][bank][:, r, :])
 
+        def layer1_part(u, bank, r0, r1):
+            for r in range(r0, r1):
+                product(u, r, z_ps[STEPS[u][0]][bank][:, r, :])
+
         def layer1_pair(u, pair):
             for e in range(2):
                 product(u, 2 * pair + e, z_ps[STEPS[u][0]][pair][:, e, :])
@@ -194,8 +198,8 @@ def tile_rows_gmlp_gelu_kernel(tc, x, w1, hs, w2, out):
             load_x(1)
             load_hs()
             load_x(2)
-            load_w2(0)
             load_w2(1)
+            load_w2(0)
             V.memset(warm[:, 0:1], 0.0)
             S.activation(out=warm[:, 1:2], in_=warm[:, 0:1], func=GELU)
             cast_w1(V, 0, 0, 4)
@@ -210,65 +214,63 @@ def tile_rows_gmlp_gelu_kernel(tc, x, w1, hs, w2, out):
             quant_w1(2, 4)
             layer1_pair(0, 1)
             layer1(1, 0)
-            cast_x(V, 128, 256)
-            cast_x(S, 256, 320)
-            cast_x(V, 320, 384)
+            cast_x(S, 128, 192)
+            cast_x(V, 192, 256)
             quant_x(1, 2)
+            layer1(2, 1)
             gelu_pair(0, 0)
-            layer1(2, 0)
-            layer1(3, 1)
+            layer1(3, 0)
             gelu_pair(0, 1)
-            quant_x(2, 3)
-            layer1(4, 1)
+            cast_x(V, 256, 512)
             gelu(1, 0)
-            cast_x(V, 384, 512)
             scale_pairs(0)
-            quant_x(3, 4)
+            quant_x(2, 4)
+            layer1(4, 0)
             scale(1)
-            gelu(2, 0)
-            layer1(5, 0)
-            layer1(6, 0)
-            gelu(3, 1)
-            layer1(7, 1)
-            cast_w2(V, 0, 0, 256)
-            cast_w2(S, 1, 0, 256)
+            gelu(2, 1)
+            layer1(5, 1)
+            layer1(6, 1)
+            gelu(3, 0)
+            layer1(7, 0)
+            cast_w2(V, 1, 0, 256)
+            cast_w2(S, 0, 0, 256)
             scale(2)
             scale(3)
-            gelu(4, 1)
+            gelu(4, 0)
             quant_l2(0, 512)
-            layer2(0, 0)
+            layer2(1, 0)
             layer2(2, 0)
-            gelu(5, 0)
+            gelu(5, 1)
             quant_l2(512, 1024)
-            layer2(1, 1)
+            layer2(0, 1)
             layer2(3, 1)
-            gelu(6, 0)
+            gelu(6, 1)
             scale(4)
-            evac(S, 0, 0, 0, 2)
+            gelu(7, 0)
+            evac(S, 0, 1, 0, 2)
             store(0)
-            gelu(7, 1)
             scale(5)
-            evac(S, 1, 1, 0, 2)
+            evac(S, 1, 0, 0, 2)
             store(1)
             quant_h(4)
             layer2(4, 2)
             scale(6)
             quant_h(5)
             layer2(5, 3)
-            evac(S, 2, 0, 2)
+            evac(S, 2, 1, 2)
             store(2)
             scale(7, 0, 64)
             quant_h(6)
             layer2(6, 0)
-            evac(S, 3, 0, 3)
+            evac(S, 3, 1, 3)
             store(3)
             scale(7, 64, 128)
-            evac(S, 0, 1, 2)
+            evac(S, 0, 0, 2)
             store(4)
             quant_h(7, 0, 64)
             quant_h(7, 64, 128)
             layer2(7, 1, 2)
-            evac(S, 1, 1, 3, 1, 0, 1)
-            evac(V, 2, 1, 3, 1, 1, 2)
+            evac(S, 1, 0, 3, 1, 0, 1)
+            evac(V, 2, 0, 3, 1, 1, 2)
             store(5)
             store(6)

@@ -17,9 +17,9 @@ PACK = 4
 ROWS = D // PACK
 CW = 128
 RUN = 4
-X_PIECES = [(0, 128), (128, 256), (256, 512)]
+X_PIECES = [(0, 128), (128, 256), (256, 384), (384, 512)]
 STEPS = [(0, 0), (1, 0), (1, 1), (0, 1), (1, 2), (1, 3), (0, 2), (0, 3)]
-STORES = [(1, 0, 2, 0, 2), (0, 0, 2, 0, 2), (1, 2, 1, 0, 2), (1, 3, 1, 0, 2), (0, 2, 1, 0, 2), (0, 3, 1, 0, 1), (0, 3, 1, 1, 2)]
+STORES = [(1, 0, 2, 0, 1), (1, 0, 2, 1, 2), (0, 0, 2, 0, 1), (0, 0, 2, 1, 2), (1, 2, 1, 0, 2), (1, 3, 1, 0, 2), (0, 2, 1, 0, 2), (0, 3, 1, 0, 1), (0, 3, 1, 1, 2)]
 W2_AT = [768, 0]
 H_AT = [512, 256, 384, 640, 1024, 1152, 1280, 1408]
 L2_WORDS = G * M + len(STEPS) * CW
@@ -196,8 +196,9 @@ def tile_rows_gmlp_gelu_kernel(tc, x, w1, hs, w2, out):
             load_w1(1)
             load_x(0)
             load_x(1)
-            load_hs()
             load_x(2)
+            load_x(3)
+            load_hs()
             load_w2(1)
             load_w2(0)
             V.memset(warm[:, 0:1], 0.0)
@@ -216,15 +217,17 @@ def tile_rows_gmlp_gelu_kernel(tc, x, w1, hs, w2, out):
             layer1(1, 0)
             cast_x(S, 128, 192)
             cast_x(V, 192, 256)
+            cast_x(V, 256, 384)
             quant_x(1, 2)
             layer1(2, 1)
             gelu_pair(0, 0)
             layer1(3, 0)
             gelu_pair(0, 1)
-            cast_x(V, 256, 512)
+            cast_x(V, 384, 512)
+            quant_x(2, 3)
             gelu(1, 0)
             scale_pairs(0)
-            quant_x(2, 4)
+            quant_x(3, 4)
             layer1(4, 0)
             scale(1)
             gelu(2, 1)
@@ -232,7 +235,8 @@ def tile_rows_gmlp_gelu_kernel(tc, x, w1, hs, w2, out):
             layer1(6, 1)
             gelu(3, 0)
             layer1(7, 0)
-            cast_w2(V, 1, 0, 256)
+            cast_w2(V, 1, 32, 256)
+            cast_w2(S, 1, 0, 32)
             cast_w2(S, 0, 0, 256)
             scale(2)
             scale(3)
@@ -246,31 +250,35 @@ def tile_rows_gmlp_gelu_kernel(tc, x, w1, hs, w2, out):
             layer2(3, 1)
             gelu(6, 1)
             scale(4)
-            gelu(7, 0)
-            evac(S, 0, 1, 0, 2)
+            evac(S, 0, 1, 0, 2, 0, 1)
             store(0)
-            scale(5)
-            evac(S, 1, 0, 0, 2)
+            gelu(7, 0)
+            evac(S, 0, 1, 0, 2, 1, 2)
             store(1)
+            scale(5)
+            evac(S, 1, 0, 0, 2, 0, 1)
+            store(2)
+            evac(S, 1, 0, 0, 2, 1, 2)
+            store(3)
             quant_h(4)
             layer2(4, 2)
             scale(6)
             quant_h(5)
             layer2(5, 3)
             evac(S, 2, 1, 2)
-            store(2)
+            store(4)
             scale(7, 0, 64)
             quant_h(6)
             layer2(6, 0)
             evac(S, 3, 1, 3)
-            store(3)
+            store(5)
             scale(7, 64, 128)
             evac(S, 0, 0, 2)
-            store(4)
+            store(6)
             quant_h(7, 0, 64)
             quant_h(7, 64, 128)
             layer2(7, 1, 2)
             evac(S, 1, 0, 3, 1, 0, 1)
             evac(V, 2, 0, 3, 1, 1, 2)
-            store(5)
-            store(6)
+            store(7)
+            store(8)

@@ -19,7 +19,7 @@ CW = 128
 RUN = 4
 X_PIECES = [(0, 128), (128, 256), (256, 384), (384, 512)]
 STEPS = [(0, 0), (1, 0), (1, 1), (0, 1), (1, 2), (1, 3), (0, 2), (0, 3)]
-STORES = [(1, 0, 2, 0, 1), (1, 0, 2, 1, 2), (0, 0, 2, 0, 1), (0, 0, 2, 1, 2), (1, 2, 1, 0, 2), (1, 3, 1, 0, 2), (0, 2, 1, 0, 2), (0, 3, 1, 0, 1), (0, 3, 1, 1, 2)]
+STORES = [(1, 0, 2, 0, 2), (0, 0, 2, 0, 2), (1, 2, 1, 0, 2), (1, 3, 1, 0, 2), (0, 2, 1, 0, 2), (0, 3, 1, 0, 1), (0, 3, 1, 1, 2)]
 W2_AT = [768, 0]
 H_AT = [512, 256, 384, 640, 1024, 1152, 1280, 1408]
 L2_WORDS = G * M + len(STEPS) * CW
@@ -235,8 +235,8 @@ def tile_rows_gmlp_gelu_kernel(tc, x, w1, hs, w2, out):
             layer1(6, 1)
             gelu(3, 0)
             layer1(7, 0)
-            cast_w2(V, 1, 32, 256)
-            cast_w2(S, 1, 0, 32)
+            cast_w2(V, 1, 16, 256)
+            cast_w2(S, 1, 0, 16)
             cast_w2(S, 0, 0, 256)
             scale(2)
             scale(3)
@@ -250,35 +250,31 @@ def tile_rows_gmlp_gelu_kernel(tc, x, w1, hs, w2, out):
             layer2(3, 1)
             gelu(6, 1)
             scale(4)
-            evac(S, 0, 1, 0, 2, 0, 1)
-            store(0)
             gelu(7, 0)
-            evac(S, 0, 1, 0, 2, 1, 2)
-            store(1)
+            evac(S, 0, 1, 0, 2)
+            store(0)
             scale(5)
-            evac(S, 1, 0, 0, 2, 0, 1)
-            store(2)
-            evac(S, 1, 0, 0, 2, 1, 2)
-            store(3)
+            evac(S, 1, 0, 0, 2)
+            store(1)
             quant_h(4)
             layer2(4, 2)
             scale(6)
             quant_h(5)
             layer2(5, 3)
             evac(S, 2, 1, 2)
-            store(4)
+            store(2)
             scale(7, 0, 64)
             quant_h(6)
             layer2(6, 0)
             evac(S, 3, 1, 3)
-            store(5)
+            store(3)
             scale(7, 64, 128)
             evac(S, 0, 0, 2)
-            store(6)
+            store(4)
             quant_h(7, 0, 64)
             quant_h(7, 64, 128)
             layer2(7, 1, 2)
             evac(S, 1, 0, 3, 1, 0, 1)
             evac(V, 2, 0, 3, 1, 1, 2)
-            store(7)
-            store(8)
+            store(5)
+            store(6)

@@ -215,8 +215,7 @@ def tile_rows_gmlp_gelu_kernel(tc, x, w1, hs, w2, out):
             quant_w1(2, 4)
             layer1_pair(0, 1)
             layer1(1, 0)
-            cast_x(S, 128, 192)
-            cast_x(V, 192, 256)
+            cast_x(S, 128, 256)
             cast_x(V, 256, 384)
             quant_x(1, 2)
             layer1(2, 1)
@@ -229,16 +228,14 @@ def tile_rows_gmlp_gelu_kernel(tc, x, w1, hs, w2, out):
             scale_pairs(0)
             quant_x(3, 4)
             layer1(4, 0)
-            scale(1)
             gelu(2, 1)
             layer1(5, 1)
             layer1(6, 1)
             gelu(3, 0)
             layer1(7, 0)
-            cast_w2(V, 1, 16, 256)
-            cast_w2(S, 1, 0, 16)
+            cast_w2(V, 1, 0, 256)
             cast_w2(S, 0, 0, 256)
-            scale(2)
+            scale_two(1)
             scale(3)
             gelu(4, 0)
             quant_l2(0, 512)
@@ -265,16 +262,16 @@ def tile_rows_gmlp_gelu_kernel(tc, x, w1, hs, w2, out):
             store(2)
             scale(7, 0, 64)
             quant_h(6)
-            layer2(6, 0)
+            layer2(6, 1)
             evac(S, 3, 1, 3)
             store(3)
             scale(7, 64, 128)
-            evac(S, 0, 0, 2)
+            evac(S, 1, 0, 2)
             store(4)
             quant_h(7, 0, 64)
             quant_h(7, 64, 128)
-            layer2(7, 1, 2)
-            evac(S, 1, 0, 3, 1, 0, 1)
+            layer2(7, 0, 2)
+            evac(S, 0, 0, 3, 1, 0, 1)
             evac(V, 2, 0, 3, 1, 1, 2)
             store(5)
             store(6)

@@ -146,9 +146,9 @@ def tile_rows_gmlp_gelu_kernel(tc, x, w1, hs, w2, out):
             S.activation(out=step_of(act, u).rearrange("p (n r) -> p n r", r=PACK)[:, lo:hi, :],
                          in_=z_ps[STEPS[u][0]][bank][:].rearrange("p r n -> p n r")[:, lo:hi, :], func=GELU)
 
-        def gelu_pair(u, pair):
-            S.activation(out=step_of(act, u).rearrange("p (h n e) -> p h n e", h=2, e=2)[:, pair, :, :],
-                         in_=z_ps[STEPS[u][0]][pair][:, 0:2, :].rearrange("p e n -> p n e"), func=GELU)
+        def gelu_pair(u, pair, lo=0, hi=CW):
+            S.activation(out=step_of(act, u).rearrange("p (h n e) -> p h n e", h=2, e=2)[:, pair, lo:hi, :],
+                         in_=z_ps[STEPS[u][0]][pair][:, 0:2, lo:hi].rearrange("p e n -> p n e"), func=GELU)
 
         def scale(u, lo=0, hi=CW):
             V.tensor_tensor(
@@ -221,19 +221,22 @@ def tile_rows_gmlp_gelu_kernel(tc, x, w1, hs, w2, out):
             layer1(2, 1)
             gelu_pair(0, 0)
             layer1(3, 0)
-            gelu_pair(0, 1)
+            gelu_pair(0, 1, 0, 64)
+            gelu_pair(0, 1, 64, 128)
             cast_x(V, 384, 512)
             quant_x(2, 3)
             gelu(1, 0)
-            scale_pairs(0)
+            scale_pairs(0, 0, 64)
             quant_x(3, 4)
+            scale_pairs(0, 64, 128)
             layer1(4, 0)
             gelu(2, 1)
             layer1(5, 1)
             layer1(6, 1)
             gelu(3, 0)
             layer1(7, 0)
-            cast_w2(V, 1, 0, 256)
+            cast_w2(V, 1, 32, 256)
+            cast_w2(S, 1, 0, 32)
             cast_w2(S, 0, 0, 256)
             scale_two(1)
             scale(3)

@@ -216,15 +216,16 @@ def tile_rows_gmlp_gelu_kernel(tc, x, w1, hs, w2, out):
             layer1_pair(0, 1)
             layer1(1, 0)
             cast_x(S, 128, 256)
-            cast_x(V, 256, 384)
+            cast_x(S, 256, 304)
+            cast_x(V, 304, 384)
             quant_x(1, 2)
             layer1(2, 1)
             gelu_pair(0, 0)
             layer1(3, 0)
             gelu_pair(0, 1, 0, 64)
             gelu_pair(0, 1, 64, 128)
-            cast_x(V, 384, 512)
             quant_x(2, 3)
+            cast_x(V, 384, 512)
             gelu(1, 0)
             scale_pairs(0, 0, 64)
             quant_x(3, 4)
@@ -250,9 +251,10 @@ def tile_rows_gmlp_gelu_kernel(tc, x, w1, hs, w2, out):
             layer2(3, 1)
             gelu(6, 1)
             scale(4)
-            gelu(7, 0)
+            gelu(7, 0, 0, 64)
             evac(S, 0, 1, 0, 2)
             store(0)
+            gelu(7, 0, 64, 128)
             scale(5)
             evac(S, 1, 0, 0, 2)
             store(1)

@@ -231,6 +231,7 @@ def tile_rows_gmlp_gelu_kernel(tc, x, w1, hs, w2, out):
             quant_x(3, 4)
             scale_pairs(0, 64, 128)
             layer1(4, 0)
+            scale(1)
             gelu(2, 1)
             layer1(5, 1)
             layer1(6, 1)
@@ -239,7 +240,7 @@ def tile_rows_gmlp_gelu_kernel(tc, x, w1, hs, w2, out):
             cast_w2(V, 1, 32, 256)
             cast_w2(S, 1, 0, 32)
             cast_w2(S, 0, 0, 256)
-            scale_two(1)
+            scale(2)
             scale(3)
             gelu(4, 0)
             quant_l2(0, 512)

@@ -211,10 +211,15 @@ def tile_rows_gmlp_gelu_kernel(tc, x, w1, hs, w2, out):
             cast_x(V, 48, 128)
             quant_w1(0, 2)
             quant_x(0, 1)
-            layer1_pair(0, 0)
+            product(0, 0, z_ps[0][0][:, 0, :])
+            product(1, 0, z_ps[1][0][:, 0, :])
+            product(0, 1, z_ps[0][0][:, 1, :])
+            product(1, 1, z_ps[1][0][:, 1, :])
             quant_w1(2, 4)
-            layer1_pair(0, 1)
-            layer1(1, 0)
+            product(0, 2, z_ps[0][1][:, 0, :])
+            product(1, 2, z_ps[1][0][:, 2, :])
+            product(0, 3, z_ps[0][1][:, 1, :])
+            product(1, 3, z_ps[1][0][:, 3, :])
             cast_x(S, 128, 256)
             cast_x(S, 256, 304)
             cast_x(V, 304, 384)

@@ -135,6 +135,11 @@ def tile_rows_gmlp_gelu_kernel(tc, x, w1, hs, w2, out):
             for r in range(r0, r1):
                 product(u, r, z_ps[STEPS[u][0]][bank][:, r, :])
 
+        def layer1_two(u, bank_u, v, bank_v):
+            for r in range(PACK):
+                product(u, r, z_ps[STEPS[u][0]][bank_u][:, r, :])
+                product(v, r, z_ps[STEPS[v][0]][bank_v][:, r, :])
+
         def layer1_pair(u, pair):
             for e in range(2):
                 product(u, 2 * pair + e, z_ps[STEPS[u][0]][pair][:, e, :])
@@ -224,9 +229,8 @@ def tile_rows_gmlp_gelu_kernel(tc, x, w1, hs, w2, out):
             cast_x(S, 256, 304)
             cast_x(V, 304, 384)
             quant_x(1, 2)
-            layer1(2, 1)
             gelu_pair(0, 0)
-            layer1(3, 0)
+            layer1_two(2, 1, 3, 0)
             gelu_pair(0, 1, 0, 64)
             gelu_pair(0, 1, 64, 128)
             quant_x(2, 3)
@@ -235,13 +239,11 @@ def tile_rows_gmlp_gelu_kernel(tc, x, w1, hs, w2, out):
             scale_pairs(0, 0, 64)
             quant_x(3, 4)
             scale_pairs(0, 64, 128)
-            layer1(4, 0)
+            layer1_two(4, 0, 6, 1)
             scale(1)
             gelu(2, 1)
-            layer1(5, 1)
-            layer1(6, 1)
             gelu(3, 0)
-            layer1(7, 0)
+            layer1_two(5, 1, 7, 0)
             cast_w2(V, 1, 32, 256)
             cast_w2(S, 1, 0, 32)
             cast_w2(S, 0, 0, 256)

@@ -229,8 +229,9 @@ def tile_rows_gmlp_gelu_kernel(tc, x, w1, hs, w2, out):
             cast_x(S, 256, 304)
             cast_x(V, 304, 384)
             quant_x(1, 2)
+            layer1(2, 1)
             gelu_pair(0, 0)
-            layer1_two(2, 1, 3, 0)
+            layer1(3, 0)
             gelu_pair(0, 1, 0, 64)
             gelu_pair(0, 1, 64, 128)
             quant_x(2, 3)
@@ -244,8 +245,8 @@ def tile_rows_gmlp_gelu_kernel(tc, x, w1, hs, w2, out):
             gelu(2, 1)
             gelu(3, 0)
             layer1_two(5, 1, 7, 0)
-            cast_w2(V, 1, 32, 256)
-            cast_w2(S, 1, 0, 32)
+            cast_w2(V, 1, 64, 256)
+            cast_w2(S, 1, 0, 64)
             cast_w2(S, 0, 0, 256)
             scale(2)
             scale(3)

@@ -247,19 +247,19 @@ def tile_rows_gmlp_gelu_kernel(tc, x, w1, hs, w2, out):
             layer1_two(5, 1, 7, 0)
             cast_w2(V, 1, 64, 256)
             cast_w2(S, 1, 0, 64)
-            cast_w2(S, 0, 0, 256)
             scale(2)
             scale(3)
             gelu(4, 0)
+            cast_w2(S, 0, 0, 256)
             quant_l2(0, 512)
             layer2(1, 0)
             layer2(2, 0)
             gelu(5, 1)
+            scale(4)
             quant_l2(512, 1024)
             layer2(0, 1)
             layer2(3, 1)
             gelu(6, 1)
-            scale(4)
             gelu(7, 0, 0, 64)
             evac(S, 0, 1, 0, 2)
             store(0)

@@ -187,6 +187,17 @@ def tile_rows_gmlp_gelu_kernel(tc, x, w1, hs, w2, out):
                     rhs=l2_q[:, cols].bitcast(FP8X4), rhs_scale=l2_s[:, cols],
                     start=True, stop=True)
 
+        def keep_warm(u, count):
+            g = STEPS[u][0]
+            cols = slice(H_AT[u], H_AT[u] + CW)
+            ms = slice(W2_AT[g], W2_AT[g] + P)
+            for i in range(count):
+                nc.tensor.matmul_mx(
+                    out=y_ps[0][:, 1, 0:CW],
+                    lhsT=l2_q[:, ms].bitcast(FP8X4), lhsT_scale=l2_s[:, ms],
+                    rhs=l2_q[:, cols].bitcast(FP8X4), rhs_scale=l2_s[:, cols],
+                    start=True, stop=True)
+
         def evac(eng, bank, g, c, chunks=1, t0=0, t1=2):
             lo = (c % 2) * CW
             s = [s for s in STORES if s[0] == g and s[1] <= c < s[1] + s[2] and s[3] <= t0 < s[4]][0]
@@ -269,9 +280,11 @@ def tile_rows_gmlp_gelu_kernel(tc, x, w1, hs, w2, out):
             store(1)
             quant_h(4)
             layer2(4, 2)
+            keep_warm(4, 3)
             scale(6)
             quant_h(5)
             layer2(5, 3)
+            keep_warm(5, 1)
             evac(S, 2, 1, 2)
             store(2)
             scale(7, 0, 64)

@@ -19,7 +19,7 @@ CW = 128
 RUN = 4
 X_PIECES = [(0, 128), (128, 256), (256, 384), (384, 512)]
 STEPS = [(0, 0), (1, 0), (1, 1), (0, 1), (1, 2), (1, 3), (0, 2), (0, 3)]
-STORES = [(1, 0, 2, 0, 2), (0, 0, 2, 0, 2), (1, 2, 1, 0, 2), (1, 3, 1, 0, 2), (0, 2, 1, 0, 2), (0, 3, 1, 0, 1), (0, 3, 1, 1, 2)]
+STORES = [(0, 256, 2, 4), (0, 256, 0, 1), (0, 256, 1, 2), (256, 384, 2, 4), (384, 512, 2, 4), (256, 384, 0, 2), (384, 512, 0, 2)]
 W2_AT = [768, 0]
 H_AT = [512, 256, 384, 640, 1024, 1152, 1280, 1408]
 L2_WORDS = G * M + len(STEPS) * CW
@@ -50,13 +50,13 @@ def tile_rows_gmlp_gelu_kernel(tc, x, w1, hs, w2, out):
         l2_bf = tile("l2_bf", [P, L2_WORDS * PACK], BF16)
         l2_q = tile("l2_q", [P, L2_WORDS], U32)
         l2_s = tile("l2_s", [P, L2_WORDS], U8)
-        y_sb = {s: tile("y_sb%d" % i, [P, s[4] - s[3], s[2] * CW], F32) for i, s in enumerate(STORES)}
+        y_sb = [tile("y_sb%d" % i, [P, s[3] - s[2], s[1] - s[0]], F32) for i, s in enumerate(STORES)]
         z_ps = [[ps.tile([P, PACK, CW], F32, name="z_ps%d_%d" % (g, b)) for b in range(2)] for g in range(G)]
         y_ps = [ps.tile([P, 2, 2 * CW], F32, name="y_ps%d" % b) for b in range(4)]
 
         x_v = x.rearrange("g (p j) n -> (g p) j n", j=PACK)
         w1_v = w1.rearrange("g (p j) k -> (g p) j k", j=PACK)
-        out_v = out.rearrange("g (t p) n -> g p t n", p=P)
+        out_v = out.rearrange("g (t p) n -> p (g t) n", p=P)
 
         def copy(eng, dst, src):
             if eng is S:
@@ -110,11 +110,8 @@ def tile_rows_gmlp_gelu_kernel(tc, x, w1, hs, w2, out):
         def quant_h(u, lo=0, hi=CW):
             quant_l2(H_AT[u] + lo, H_AT[u] + hi)
 
-        def quant_w2(g):
-            quant_l2(W2_AT[g], W2_AT[g] + M)
-
-        def h_of(u, steps=1):
-            return l2_bf[:, PACK * H_AT[u]:PACK * (H_AT[u] + steps * CW)]
+        def h_of(u):
+            return l2_bf[:, PACK * H_AT[u]:PACK * (H_AT[u] + CW)]
 
         def product(u, r, dst):
             g, c = STEPS[u]
@@ -131,18 +128,15 @@ def tile_rows_gmlp_gelu_kernel(tc, x, w1, hs, w2, out):
             for r in range(PACK):
                 product(u, r, z_ps[STEPS[u][0]][bank][:, r, :])
 
-        def layer1_part(u, bank, r0, r1):
-            for r in range(r0, r1):
-                product(u, r, z_ps[STEPS[u][0]][bank][:, r, :])
-
         def layer1_two(u, bank_u, v, bank_v):
             for r in range(PACK):
                 product(u, r, z_ps[STEPS[u][0]][bank_u][:, r, :])
                 product(v, r, z_ps[STEPS[v][0]][bank_v][:, r, :])
 
-        def layer1_pair(u, pair):
+        def layer1_first(pair):
             for e in range(2):
-                product(u, 2 * pair + e, z_ps[STEPS[u][0]][pair][:, e, :])
+                product(0, 2 * pair + e, z_ps[STEPS[0][0]][pair][:, e, :])
+                product(1, 2 * pair + e, z_ps[STEPS[1][0]][0][:, 2 * pair + e, :])
 
         def step_of(t, u):
             return t[:, u * CW * PACK:(u + 1) * CW * PACK]
@@ -162,13 +156,6 @@ def tile_rows_gmlp_gelu_kernel(tc, x, w1, hs, w2, out):
                 in1=hs_t[:, STEPS[u][0], 0:PACK].unsqueeze(1).to_broadcast([P, hi - lo, PACK]),
                 op=mybir.AluOpType.mult)
 
-        def scale_two(u):
-            V.tensor_tensor(
-                out=h_of(u, 2).rearrange("p (n r) -> p n r", r=PACK),
-                in0=act[:, u * CW * PACK:(u + 2) * CW * PACK].rearrange("p (n r) -> p n r", r=PACK),
-                in1=hs_t[:, STEPS[u][0], 0:PACK].unsqueeze(1).to_broadcast([P, 2 * CW, PACK]),
-                op=mybir.AluOpType.mult)
-
         def scale_pairs(u, lo=0, hi=CW):
             V.tensor_tensor(
                 out=h_of(u).rearrange("p (n h e) -> p n h e", h=2, e=2)[:, lo:hi, :, :],
@@ -176,36 +163,41 @@ def tile_rows_gmlp_gelu_kernel(tc, x, w1, hs, w2, out):
                 in1=hs_t[:, STEPS[u][0], 0:PACK].rearrange("p (h e) -> p h e", h=2).unsqueeze(1).to_broadcast([P, hi - lo, 2, 2]),
                 op=mybir.AluOpType.mult)
 
-        def layer2(u, bank0, bank1=None):
+        def half2(u, t, bank):
             g, c = STEPS[u]
             cols = slice(H_AT[u], H_AT[u] + CW)
-            for t, bank in enumerate((bank0, bank0 if bank1 is None else bank1)):
-                ms = slice(W2_AT[g] + t * P, W2_AT[g] + (t + 1) * P)
-                nc.tensor.matmul_mx(
-                    out=y_ps[bank][:, t, (c % 2) * CW:(c % 2 + 1) * CW],
-                    lhsT=l2_q[:, ms].bitcast(FP8X4), lhsT_scale=l2_s[:, ms],
-                    rhs=l2_q[:, cols].bitcast(FP8X4), rhs_scale=l2_s[:, cols],
-                    start=True, stop=True)
+            ms = slice(W2_AT[g] + t * P, W2_AT[g] + (t + 1) * P)
+            nc.tensor.matmul_mx(
+                out=y_ps[bank][:, t, (c % 2) * CW:(c % 2 + 1) * CW],
+                lhsT=l2_q[:, ms].bitcast(FP8X4), lhsT_scale=l2_s[:, ms],
+                rhs=l2_q[:, cols].bitcast(FP8X4), rhs_scale=l2_s[:, cols],
+                start=True, stop=True)
+
+        def layer2(u, bank0, bank1):
+            half2(u, 0, bank0)
+            half2(u, 1, bank1)
+
+        def evac(eng, bank, g, lo, hi, t0=0, t1=2):
+            first = 2 * g + t0
+            i = [i for i, s in enumerate(STORES) if s[0] <= lo < s[1] and s[2] <= first < s[3]][0]
+            s = STORES[i]
+            at = lo % (2 * CW)
+            copy(eng, y_sb[i][:, first - s[2]:first - s[2] + t1 - t0, lo - s[0]:hi - s[0]],
+                 y_ps[bank][:, t0:t1, at:at + hi - lo])
+
+        def store(i, q=nc.sync):
+            lo, hi, h0, h1 = STORES[i]
+            q.dma_start(out=out_v[:, h0:h1, lo:hi], in_=y_sb[i][:])
 
         def keep_warm(u, count):
-            g = STEPS[u][0]
             cols = slice(H_AT[u], H_AT[u] + CW)
-            ms = slice(W2_AT[g], W2_AT[g] + P)
+            ms = slice(W2_AT[STEPS[u][0]], W2_AT[STEPS[u][0]] + P)
             for i in range(count):
                 nc.tensor.matmul_mx(
                     out=y_ps[0][:, 1, 0:CW],
                     lhsT=l2_q[:, ms].bitcast(FP8X4), lhsT_scale=l2_s[:, ms],
                     rhs=l2_q[:, cols].bitcast(FP8X4), rhs_scale=l2_s[:, cols],
                     start=True, stop=True)
-
-        def evac(eng, bank, g, c, chunks=1, t0=0, t1=2):
-            lo = (c % 2) * CW
-            s = [s for s in STORES if s[0] == g and s[1] <= c < s[1] + s[2] and s[3] <= t0 < s[4]][0]
-            copy(eng, y_sb[s][:, t0 - s[3]:t1 - s[3], (c - s[1]) * CW:(c - s[1] + chunks) * CW], y_ps[bank][:, t0:t1, lo:lo + chunks * CW])
-
-        def store(i, q=nc.sync):
-            g, c, chunks, t0, t1 = STORES[i]
-            q.dma_start(out=out_v[g][:, t0:t1, c * CW:(c + chunks) * CW], in_=y_sb[STORES[i]][:])
 
         with tc.manual_schedule():
             load_w1(0)
@@ -227,15 +219,9 @@ def tile_rows_gmlp_gelu_kernel(tc, x, w1, hs, w2, out):
             cast_x(V, 48, 128)
             quant_w1(0, 2)
             quant_x(0, 1)
-            product(0, 0, z_ps[0][0][:, 0, :])
-            product(1, 0, z_ps[1][0][:, 0, :])
-            product(0, 1, z_ps[0][0][:, 1, :])
-            product(1, 1, z_ps[1][0][:, 1, :])
+            layer1_first(0)
             quant_w1(2, 4)
-            product(0, 2, z_ps[0][1][:, 0, :])
-            product(1, 2, z_ps[1][0][:, 2, :])
-            product(0, 3, z_ps[0][1][:, 1, :])
-            product(1, 3, z_ps[1][0][:, 3, :])
+            layer1_first(1)
             cast_x(S, 128, 256)
             cast_x(S, 256, 304)
             cast_x(V, 304, 384)
@@ -263,42 +249,42 @@ def tile_rows_gmlp_gelu_kernel(tc, x, w1, hs, w2, out):
             gelu(4, 0)
             cast_w2(S, 0, 0, 256)
             quant_l2(0, 512)
-            layer2(1, 0)
-            layer2(2, 0)
+            layer2(1, 0, 0)
+            layer2(2, 0, 0)
             gelu(5, 1)
             scale(4)
             quant_l2(512, 1024)
-            layer2(0, 1)
-            layer2(3, 1)
+            layer2(0, 1, 1)
+            layer2(3, 1, 1)
             gelu(6, 1)
-            gelu(7, 0, 0, 64)
-            evac(S, 0, 1, 0, 2)
+            evac(S, 0, 1, 0, 256)
             store(0)
+            gelu(7, 0, 0, 64)
             gelu(7, 0, 64, 128)
             scale(5)
-            evac(S, 1, 0, 0, 2)
+            evac(S, 1, 0, 0, 256, 0, 1)
             store(1)
+            evac(S, 1, 0, 0, 256, 1, 2)
+            store(2)
             quant_h(4)
-            layer2(4, 2)
+            layer2(4, 2, 2)
             keep_warm(4, 3)
             scale(6)
             quant_h(5)
-            layer2(5, 3)
-            keep_warm(5, 1)
-            evac(S, 2, 1, 2)
-            store(2)
+            layer2(5, 3, 3)
+            evac(S, 2, 1, 256, 384)
+            store(3)
             scale(7, 0, 64)
             quant_h(6)
-            layer2(6, 1)
-            evac(S, 3, 1, 3)
-            store(3)
-            scale(7, 64, 128)
-            evac(S, 1, 0, 2)
+            layer2(6, 1, 1)
+            evac(S, 3, 1, 384, 512)
             store(4)
+            scale(7, 64, 128)
+            evac(S, 1, 0, 256, 384)
+            store(5)
             quant_h(7, 0, 64)
             quant_h(7, 64, 128)
             layer2(7, 0, 2)
-            evac(S, 0, 0, 3, 1, 0, 1)
-            evac(V, 2, 0, 3, 1, 1, 2)
-            store(5)
+            evac(S, 0, 0, 384, 512, 0, 1)
+            evac(V, 2, 0, 384, 512, 1, 2)
             store(6)

@@ -205,8 +205,8 @@ def tile_rows_gmlp_gelu_kernel(tc, x, w1, hs, w2, out):
             load_x(0)
             load_x(1)
             load_x(2)
-            load_x(3)
             load_hs()
+            load_x(3)
             load_w2(1)
             load_w2(0)
             V.memset(warm[:, 0:1], 0.0)
@@ -276,15 +276,15 @@ def tile_rows_gmlp_gelu_kernel(tc, x, w1, hs, w2, out):
             store(3)
             scale(7, 0, 64)
             quant_h(6)
-            layer2(6, 1, 1)
+            layer2(6, 0, 0)
             evac(S, 3, 1, 384, 512)
             store(4)
             scale(7, 64, 128)
-            evac(S, 1, 0, 256, 384)
+            evac(S, 0, 0, 256, 384)
             store(5)
             quant_h(7, 0, 64)
             quant_h(7, 64, 128)
-            layer2(7, 0, 2)
-            evac(S, 0, 0, 384, 512, 0, 1)
+            layer2(7, 1, 2)
+            evac(S, 1, 0, 384, 512, 0, 1)
             evac(V, 2, 0, 384, 512, 1, 2)
             store(6)

@@ -20,8 +20,8 @@ RUN = 4
 X_PIECES = [(0, 128), (128, 256), (256, 384), (384, 512)]
 STEPS = [(0, 0), (1, 0), (1, 1), (0, 1), (1, 2), (1, 3), (0, 2), (0, 3)]
 STORES = [(0, 256, 2, 4), (0, 256, 0, 1), (0, 256, 1, 2), (256, 384, 2, 4), (384, 512, 2, 4), (256, 384, 0, 2), (384, 512, 0, 2)]
-W2_AT = [768, 0]
-H_AT = [512, 256, 384, 640, 1024, 1152, 1280, 1408]
+W2_AT = [896, 0]
+H_AT = [512, 256, 384, 640, 768, 1152, 1280, 1408]
 L2_WORDS = G * M + len(STEPS) * CW
 
 
@@ -205,8 +205,8 @@ def tile_rows_gmlp_gelu_kernel(tc, x, w1, hs, w2, out):
             load_x(0)
             load_x(1)
             load_x(2)
-            load_hs()
             load_x(3)
+            load_hs()
             load_w2(1)
             load_w2(0)
             V.memset(warm[:, 0:1], 0.0)
@@ -242,8 +242,8 @@ def tile_rows_gmlp_gelu_kernel(tc, x, w1, hs, w2, out):
             gelu(2, 1)
             gelu(3, 0)
             layer1_two(5, 1, 7, 0)
-            cast_w2(V, 1, 64, 256)
-            cast_w2(S, 1, 0, 64)
+            cast_w2(V, 1, 96, 256)
+            cast_w2(S, 1, 0, 96)
             scale(2)
             scale(3)
             gelu(4, 0)
@@ -253,21 +253,21 @@ def tile_rows_gmlp_gelu_kernel(tc, x, w1, hs, w2, out):
             layer2(2, 0, 0)
             gelu(5, 1)
             scale(4)
-            quant_l2(512, 1024)
+            quant_l2(512, 768)
+            quant_l2(768, 1152)
             layer2(0, 1, 1)
             layer2(3, 1, 1)
+            layer2(4, 2, 2)
             gelu(6, 1)
+            gelu(7, 0, 0, 64)
             evac(S, 0, 1, 0, 256)
             store(0)
-            gelu(7, 0, 0, 64)
             gelu(7, 0, 64, 128)
             scale(5)
             evac(S, 1, 0, 0, 256, 0, 1)
             store(1)
             evac(S, 1, 0, 0, 256, 1, 2)
             store(2)
-            quant_h(4)
-            layer2(4, 2, 2)
             keep_warm(4, 3)
             scale(6)
             quant_h(5)

@@ -18,8 +18,8 @@ ROWS = D // PACK
 CW = 128
 RUN = 4
 X_PIECES = [(0, 128), (128, 256), (256, 384), (384, 512)]
-STEPS = [(0, 0), (1, 0), (1, 1), (0, 1), (1, 2), (1, 3), (0, 2), (0, 3)]
-STORES = [(0, 256, 2, 4), (0, 256, 0, 1), (0, 256, 1, 2), (256, 384, 2, 4), (384, 512, 2, 4), (256, 384, 0, 2), (384, 512, 0, 2)]
+STEPS = [(0, 0), (1, 0), (1, 1), (0, 1), (0, 2), (1, 2), (1, 3), (0, 3)]
+STORES = [(0, 256, 2, 4), (0, 384, 0, 1), (0, 384, 1, 2), (256, 384, 2, 4), (384, 512, 2, 4), (384, 512, 0, 1), (384, 512, 1, 2)]
 W2_AT = [896, 0]
 H_AT = [512, 256, 384, 640, 768, 1152, 1280, 1408]
 L2_WORDS = G * M + len(STEPS) * CW
@@ -52,7 +52,7 @@ def tile_rows_gmlp_gelu_kernel(tc, x, w1, hs, w2, out):
         l2_s = tile("l2_s", [P, L2_WORDS], U8)
         y_sb = [tile("y_sb%d" % i, [P, s[3] - s[2], s[1] - s[0]], F32) for i, s in enumerate(STORES)]
         z_ps = [[ps.tile([P, PACK, CW], F32, name="z_ps%d_%d" % (g, b)) for b in range(2)] for g in range(G)]
-        y_ps = [ps.tile([P, 2, 2 * CW], F32, name="y_ps%d" % b) for b in range(4)]
+        y_ps = [ps.tile([P, PACK * CW], F32, name="y_ps%d" % b) for b in range(4)]
 
         x_v = x.rearrange("g (p j) n -> (g p) j n", j=PACK)
         w1_v = w1.rearrange("g (p j) k -> (g p) j k", j=PACK)
@@ -163,27 +163,19 @@ def tile_rows_gmlp_gelu_kernel(tc, x, w1, hs, w2, out):
                 in1=hs_t[:, STEPS[u][0], 0:PACK].rearrange("p (h e) -> p h e", h=2).unsqueeze(1).to_broadcast([P, hi - lo, 2, 2]),
                 op=mybir.AluOpType.mult)
 
-        def half2(u, t, bank):
-            g, c = STEPS[u]
+        def half2(u, t, bank, slot):
+            g = STEPS[u][0]
             cols = slice(H_AT[u], H_AT[u] + CW)
             ms = slice(W2_AT[g] + t * P, W2_AT[g] + (t + 1) * P)
             nc.tensor.matmul_mx(
-                out=y_ps[bank][:, t, (c % 2) * CW:(c % 2 + 1) * CW],
+                out=y_ps[bank][:, slot * CW:(slot + 1) * CW],
                 lhsT=l2_q[:, ms].bitcast(FP8X4), lhsT_scale=l2_s[:, ms],
                 rhs=l2_q[:, cols].bitcast(FP8X4), rhs_scale=l2_s[:, cols],
                 start=True, stop=True)
 
-        def layer2(u, bank0, bank1):
-            half2(u, 0, bank0)
-            half2(u, 1, bank1)
-
-        def evac(eng, bank, g, lo, hi, t0=0, t1=2):
-            first = 2 * g + t0
-            i = [i for i, s in enumerate(STORES) if s[0] <= lo < s[1] and s[2] <= first < s[3]][0]
-            s = STORES[i]
-            at = lo % (2 * CW)
-            copy(eng, y_sb[i][:, first - s[2]:first - s[2] + t1 - t0, lo - s[0]:hi - s[0]],
-                 y_ps[bank][:, t0:t1, at:at + hi - lo])
+        def evac(eng, bank, i, t0=0, t1=None):
+            dst = y_sb[i][:, t0:t1, :].rearrange("p t n -> p (t n)")
+            copy(eng, dst, y_ps[bank][:, 0:dst.shape[1]])
 
         def store(i, q=nc.sync):
             lo, hi, h0, h1 = STORES[i]
@@ -194,7 +186,7 @@ def tile_rows_gmlp_gelu_kernel(tc, x, w1, hs, w2, out):
             ms = slice(W2_AT[STEPS[u][0]], W2_AT[STEPS[u][0]] + P)
             for i in range(count):
                 nc.tensor.matmul_mx(
-                    out=y_ps[0][:, 1, 0:CW],
+                    out=y_ps[0][:, 3 * CW:4 * CW],
                     lhsT=l2_q[:, ms].bitcast(FP8X4), lhsT_scale=l2_s[:, ms],
                     rhs=l2_q[:, cols].bitcast(FP8X4), rhs_scale=l2_s[:, cols],
                     start=True, stop=True)
@@ -237,54 +229,61 @@ def tile_rows_gmlp_gelu_kernel(tc, x, w1, hs, w2, out):
             scale_pairs(0, 0, 64)
             quant_x(3, 4)
             scale_pairs(0, 64, 128)
-            layer1_two(4, 0, 6, 1)
+            layer1_two(5, 0, 4, 1)
             scale(1)
             gelu(2, 1)
             gelu(3, 0)
-            layer1_two(5, 1, 7, 0)
-            cast_w2(V, 1, 96, 256)
-            cast_w2(S, 1, 0, 96)
+            layer1_two(6, 1, 7, 0)
+            cast_w2(V, 1, 56, 256)
+            cast_w2(S, 1, 0, 56)
             scale(2)
             scale(3)
-            gelu(4, 0)
+            gelu(4, 1)
             cast_w2(S, 0, 0, 256)
             quant_l2(0, 512)
-            layer2(1, 0, 0)
-            layer2(2, 0, 0)
-            gelu(5, 1)
+            half2(1, 0, 0, 0)
+            half2(2, 0, 0, 1)
+            half2(1, 1, 0, 2)
+            half2(2, 1, 0, 3)
+            gelu(5, 0)
             scale(4)
             quant_l2(512, 768)
             quant_l2(768, 1152)
-            layer2(0, 1, 1)
-            layer2(3, 1, 1)
-            layer2(4, 2, 2)
+            half2(0, 0, 1, 0)
+            half2(3, 0, 1, 1)
+            half2(4, 0, 1, 2)
+            half2(0, 1, 2, 0)
+            half2(3, 1, 2, 1)
+            half2(4, 1, 2, 2)
             gelu(6, 1)
             gelu(7, 0, 0, 64)
-            evac(S, 0, 1, 0, 256)
+            evac(S, 0, 0)
             store(0)
             gelu(7, 0, 64, 128)
             scale(5)
-            evac(S, 1, 0, 0, 256, 0, 1)
+            evac(S, 1, 1)
             store(1)
-            evac(S, 1, 0, 0, 256, 1, 2)
+            evac(S, 2, 2)
             store(2)
             keep_warm(4, 3)
             scale(6)
             quant_h(5)
-            layer2(5, 3, 3)
-            evac(S, 2, 1, 256, 384)
-            store(3)
+            half2(5, 0, 3, 0)
+            half2(5, 1, 3, 1)
             scale(7, 0, 64)
             quant_h(6)
-            layer2(6, 0, 0)
-            evac(S, 3, 1, 384, 512)
-            store(4)
+            half2(6, 0, 0, 0)
+            half2(6, 1, 0, 1)
+            evac(S, 3, 3)
+            store(3)
             scale(7, 64, 128)
-            evac(S, 0, 0, 256, 384)
-            store(5)
             quant_h(7, 0, 64)
             quant_h(7, 64, 128)
-            layer2(7, 1, 2)
-            evac(S, 1, 0, 384, 512, 0, 1)
-            evac(V, 2, 0, 384, 512, 1, 2)
+            evac(S, 0, 4)
+            store(4)
+            half2(7, 0, 1, 0)
+            half2(7, 1, 2, 0)
+            evac(S, 1, 5)
+            evac(V, 2, 6)
+            store(5)
             store(6)

@@ -20,8 +20,8 @@ RUN = 4
 X_PIECES = [(0, 128), (128, 256), (256, 384), (384, 512)]
 STEPS = [(0, 0), (1, 0), (1, 1), (0, 1), (0, 2), (1, 2), (1, 3), (0, 3)]
 STORES = [(0, 256, 2, 4), (0, 384, 0, 1), (0, 384, 1, 2), (256, 384, 2, 4), (384, 512, 2, 4), (384, 512, 0, 1), (384, 512, 1, 2)]
-W2_AT = [896, 0]
-H_AT = [512, 256, 384, 640, 768, 1152, 1280, 1408]
+W2_AT = [768, 0]
+H_AT = [512, 256, 384, 640, 1024, 1152, 1280, 1408]
 L2_WORDS = G * M + len(STEPS) * CW
 
 
@@ -234,8 +234,8 @@ def tile_rows_gmlp_gelu_kernel(tc, x, w1, hs, w2, out):
             gelu(2, 1)
             gelu(3, 0)
             layer1_two(6, 1, 7, 0)
-            cast_w2(V, 1, 56, 256)
-            cast_w2(S, 1, 0, 56)
+            cast_w2(V, 1, 72, 256)
+            cast_w2(S, 1, 0, 72)
             scale(2)
             scale(3)
             gelu(4, 1)
@@ -247,8 +247,8 @@ def tile_rows_gmlp_gelu_kernel(tc, x, w1, hs, w2, out):
             half2(2, 1, 0, 3)
             gelu(5, 0)
             scale(4)
-            quant_l2(512, 768)
-            quant_l2(768, 1152)
+            quant_l2(512, 1024)
+            quant_h(4)
             half2(0, 0, 1, 0)
             half2(3, 0, 1, 1)
             half2(4, 0, 1, 2)

@@ -19,7 +19,7 @@ CW = 128
 RUN = 4
 X_PIECES = [(0, 128), (128, 256), (256, 384), (384, 512)]
 STEPS = [(0, 0), (1, 0), (1, 1), (0, 1), (0, 2), (1, 2), (1, 3), (0, 3)]
-STORES = [(0, 256, 2, 4), (0, 384, 0, 1), (0, 384, 1, 2), (256, 384, 2, 4), (384, 512, 2, 4), (384, 512, 0, 1), (384, 512, 1, 2)]
+STORES = [(0, 256, 2, 4), (0, 384, 0, 1), (0, 384, 1, 2), (256, 384, 2, 4), (384, 512, 2, 4), (384, 448, 0, 2), (448, 512, 0, 2)]
 W2_AT = [768, 0]
 H_AT = [512, 256, 384, 640, 1024, 1152, 1280, 1408]
 L2_WORDS = G * M + len(STEPS) * CW
@@ -191,6 +191,19 @@ def tile_rows_gmlp_gelu_kernel(tc, x, w1, hs, w2, out):
                     rhs=l2_q[:, cols].bitcast(FP8X4), rhs_scale=l2_s[:, cols],
                     start=True, stop=True)
 
+        def window2(lo, t, bank):
+            first = H_AT[7] + lo - 448
+            words = slice(first, first + CW)
+            ms = slice(W2_AT[0] + t * P, W2_AT[0] + (t + 1) * P)
+            nc.tensor.matmul_mx(
+                out=y_ps[bank][:, t * CW:(t + 1) * CW],
+                lhsT=l2_q[:, ms].bitcast(FP8X4), lhsT_scale=l2_s[:, ms],
+                rhs=l2_q[:, words].bitcast(FP8X4), rhs_scale=l2_s[:, words],
+                start=True, stop=True)
+
+        def evac_new(eng, bank, i):
+            copy(eng, y_sb[i][:], y_ps[bank][:, 0:2 * CW].rearrange("p (t n) -> p t n", t=2)[:, :, CW // 2:CW])
+
         with tc.manual_schedule():
             load_w1(0)
             load_w1(1)
@@ -234,8 +247,8 @@ def tile_rows_gmlp_gelu_kernel(tc, x, w1, hs, w2, out):
             gelu(2, 1)
             gelu(3, 0)
             layer1_two(6, 1, 7, 0)
-            cast_w2(V, 1, 72, 256)
-            cast_w2(S, 1, 0, 72)
+            cast_w2(V, 1, 64, 256)
+            cast_w2(S, 1, 0, 64)
             scale(2)
             scale(3)
             gelu(4, 1)
@@ -256,9 +269,9 @@ def tile_rows_gmlp_gelu_kernel(tc, x, w1, hs, w2, out):
             half2(3, 1, 2, 1)
             half2(4, 1, 2, 2)
             gelu(6, 1)
-            gelu(7, 0, 0, 64)
             evac(S, 0, 0)
             store(0)
+            gelu(7, 0, 0, 64)
             gelu(7, 0, 64, 128)
             scale(5)
             evac(S, 1, 1)
@@ -278,12 +291,14 @@ def tile_rows_gmlp_gelu_kernel(tc, x, w1, hs, w2, out):
             store(3)
             scale(7, 64, 128)
             quant_h(7, 0, 64)
+            window2(384, 0, 1)
+            window2(384, 1, 1)
             quant_h(7, 64, 128)
-            evac(S, 0, 4)
+            window2(448, 0, 2)
+            window2(448, 1, 2)
+            evac(V, 0, 4)
             store(4)
-            half2(7, 0, 1, 0)
-            half2(7, 1, 2, 0)
-            evac(S, 1, 5)
-            evac(V, 2, 6)
+            evac_new(V, 1, 5)
             store(5)
+            evac_new(V, 2, 6)
             store(6)

@@ -181,16 +181,6 @@ def tile_rows_gmlp_gelu_kernel(tc, x, w1, hs, w2, out):
             lo, hi, h0, h1 = STORES[i]
             q.dma_start(out=out_v[:, h0:h1, lo:hi], in_=y_sb[i][:])
 
-        def keep_warm(u, count):
-            cols = slice(H_AT[u], H_AT[u] + CW)
-            ms = slice(W2_AT[STEPS[u][0]], W2_AT[STEPS[u][0]] + P)
-            for i in range(count):
-                nc.tensor.matmul_mx(
-                    out=y_ps[0][:, 3 * CW:4 * CW],
-                    lhsT=l2_q[:, ms].bitcast(FP8X4), lhsT_scale=l2_s[:, ms],
-                    rhs=l2_q[:, cols].bitcast(FP8X4), rhs_scale=l2_s[:, cols],
-                    start=True, stop=True)
-
         def window2(lo, t, bank):
             first = H_AT[7] + lo - 448
             words = slice(first, first + CW)
@@ -278,7 +268,6 @@ def tile_rows_gmlp_gelu_kernel(tc, x, w1, hs, w2, out):
             store(1)
             evac(S, 2, 2)
             store(2)
-            keep_warm(4, 3)
             scale(6)
             quant_h(5)
             half2(5, 0, 3, 0)

from contextlib import ExitStack

import concourse.mybir as mybir

G, D, K, M, N = 2, 256, 512, 256, 512
FLOPS = 2 * G * N * (D * K + K * M)

F32 = mybir.dt.float32
BF16 = mybir.dt.bfloat16
U32 = mybir.dt.uint32
U8 = mybir.dt.uint8
FP8X4 = mybir.dt.float8_e4m3fn_x4
GELU = mybir.ActivationFunctionType.Gelu_apprx_tanh

P = 128
PACK = 4
ROWS = D // PACK
CW = 128
RUN = 4
X_PIECES = [(0, 128), (128, 256), (256, 384), (384, 512)]
STEPS = [(0, 0), (1, 0), (1, 1), (0, 1), (0, 2), (1, 2), (1, 3), (0, 3)]
STORES = [(0, 256, 2, 4), (0, 384, 0, 1), (0, 384, 1, 2), (256, 384, 2, 4), (384, 512, 2, 4), (384, 448, 0, 2), (448, 512, 0, 2)]
W2_AT = [768, 0]
H_AT = [512, 256, 384, 640, 1024, 1152, 1280, 1408]
L2_WORDS = G * M + len(STEPS) * CW


def tile_rows_gmlp_gelu_kernel(tc, x, w1, hs, w2, out):
    nc = tc.nc
    V, S = nc.vector, nc.scalar
    with ExitStack() as ctx:
        sb = ctx.enter_context(tc.tile_pool(name="sb", bufs=1))
        ps = ctx.enter_context(tc.psum_pool(name="ps", bufs=1))

        def tile(name, shape, dtype):
            return sb.tile(shape, dtype, name=name, align_bytes=256)

        x_raw = [tile("x_raw%d" % i, [P, PACK, hi - lo], F32) for i, (lo, hi) in enumerate(X_PIECES)]
        x_bf = tile("x_bf", [P, N * PACK], BF16)
        x_q = tile("x_q", [P, N], U32)
        x_s = tile("x_s", [P, N], U8)
        w1_raw = [tile("w1_raw%d" % i, [P, 2, K], F32) for i in range(2)]
        w1_bf = tile("w1_bf", [P, K * PACK], BF16)
        w1_q = tile("w1_q", [P, K], U32)
        w1_s = tile("w1_s", [P, K], U8)
        w2_raw = [tile("w2_raw%d" % g, [P, PACK, M], F32) for g in range(G)]
        hs_t = tile("hs_t", [P, G, 8], F32)
        warm = tile("warm", [P, 2], F32)
        act = tile("act", [P, len(STEPS) * CW * PACK], F32)
        l2_bf = tile("l2_bf", [P, L2_WORDS * PACK], BF16)
        l2_q = tile("l2_q", [P, L2_WORDS], U32)
        l2_s = tile("l2_s", [P, L2_WORDS], U8)
        y_sb = [tile("y_sb%d" % i, [P, s[3] - s[2], s[1] - s[0]], F32) for i, s in enumerate(STORES)]
        z_ps = [[ps.tile([P, PACK, CW], F32, name="z_ps%d_%d" % (g, b)) for b in range(2)] for g in range(G)]
        y_ps = [ps.tile([P, PACK * CW], F32, name="y_ps%d" % b) for b in range(4)]

        x_v = x.rearrange("g (p j) n -> (g p) j n", j=PACK)
        w1_v = w1.rearrange("g (p j) k -> (g p) j k", j=PACK)
        out_v = out.rearrange("g (t p) n -> p (g t) n", p=P)

        def copy(eng, dst, src):
            if eng is S:
                S.copy(out=dst, in_=src)
            else:
                eng.tensor_copy(out=dst, in_=src)

        def load_x(i, q=nc.sync):
            lo, hi = X_PIECES[i]
            q.dma_start(out=x_raw[i][:], in_=x_v[:, :, lo:hi])

        def load_w1(i, q=nc.sync):
            q.dma_start(out=w1_raw[i][:], in_=w1_v[:, 2 * i:2 * i + 2, :])

        def load_w2(g, q=nc.sync):
            q.dma_start(out=w2_raw[g][:], in_=w2[g].rearrange("(p j) m -> p j m", j=PACK))

        def load_hs(q=nc.sync):
            q.dma_start(out=hs_t[:, :, 0:PACK], in_=hs.rearrange("g (p r) o -> p g (r o)", r=PACK))

        def interleave(eng, dst, src):
            copy(eng, dst.rearrange("p (c i j) -> p c j i", i=RUN, j=PACK),
                 src.rearrange("p j (c i) -> p c j i", i=RUN))

        def cast_x(eng, lo, hi):
            i = max(i for i, piece in enumerate(X_PIECES) if piece[0] <= lo)
            first = X_PIECES[i][0]
            interleave(eng, x_bf[:, PACK * lo:PACK * hi], x_raw[i][:, :, lo - first:hi - first])

        def cast_w2(eng, g, lo, hi):
            interleave(eng, l2_bf[:, PACK * (W2_AT[g] + lo):PACK * (W2_AT[g] + hi)], w2_raw[g][:, :, lo:hi])

        def cast_w1(eng, half, r0, r1, lo=0, hi=P):
            copy(eng,
                 w1_bf[:].rearrange("p (r s j) -> p s j r", r=PACK, j=PACK)[:, lo:hi, 2 * half:2 * half + 2, r0:r1],
                 w1_raw[half][:].rearrange("p j (s r) -> p s j r", r=PACK)[:, lo:hi, :, r0:r1])

        def quant(codes, scales, src, lo, hi):
            V.quantize_mx(out=codes[:, lo:hi].bitcast(FP8X4), scales=scales[:, lo:hi],
                          in_=src[:, PACK * lo:PACK * hi])

        def quant_w1(r0, r1):
            quant(w1_q, w1_s, w1_bf, r0 * P, r1 * P)

        def quant_x(c0, c1):
            quant(x_q, x_s, x_bf, c0 * CW, c1 * CW)

        def quant_l2(lo, hi):
            quant(l2_q, l2_s, l2_bf, lo, hi)

        def quant_h(u, lo=0, hi=CW):
            quant_l2(H_AT[u] + lo, H_AT[u] + hi)

        def h_of(u):
            return l2_bf[:, PACK * H_AT[u]:PACK * (H_AT[u] + CW)]

        def product(u, r, dst):
            g, c = STEPS[u]
            rows = slice(ROWS * g, ROWS * (g + 1))
            cols = slice(c * CW, (c + 1) * CW)
            ks = slice(r * P, (r + 1) * P)
            nc.tensor.matmul_mx(
                out=dst,
                lhsT=w1_q[rows, ks].bitcast(FP8X4), lhsT_scale=w1_s[rows, ks],
                rhs=x_q[rows, cols].bitcast(FP8X4), rhs_scale=x_s[rows, cols],
                start=True, stop=True)

        def layer1(u, bank):
            for r in range(PACK):
                product(u, r, z_ps[STEPS[u][0]][bank][:, r, :])

        def layer1_two(u, bank_u, v, bank_v):
            for r in range(PACK):
                product(u, r, z_ps[STEPS[u][0]][bank_u][:, r, :])
                product(v, r, z_ps[STEPS[v][0]][bank_v][:, r, :])

        def layer1_first(pair):
            for e in range(2):
                product(0, 2 * pair + e, z_ps[STEPS[0][0]][pair][:, e, :])
                product(1, 2 * pair + e, z_ps[STEPS[1][0]][0][:, 2 * pair + e, :])

        def step_of(t, u):
            return t[:, u * CW * PACK:(u + 1) * CW * PACK]

        def gelu(u, bank, lo=0, hi=CW):
            S.activation(out=step_of(act, u).rearrange("p (n r) -> p n r", r=PACK)[:, lo:hi, :],
                         in_=z_ps[STEPS[u][0]][bank][:].rearrange("p r n -> p n r")[:, lo:hi, :], func=GELU)

        def gelu_pair(u, pair, lo=0, hi=CW):
            S.activation(out=step_of(act, u).rearrange("p (h n e) -> p h n e", h=2, e=2)[:, pair, lo:hi, :],
                         in_=z_ps[STEPS[u][0]][pair][:, 0:2, lo:hi].rearrange("p e n -> p n e"), func=GELU)

        def scale(u, lo=0, hi=CW):
            V.tensor_tensor(
                out=h_of(u).rearrange("p (n r) -> p n r", r=PACK)[:, lo:hi, :],
                in0=step_of(act, u).rearrange("p (n r) -> p n r", r=PACK)[:, lo:hi, :],
                in1=hs_t[:, STEPS[u][0], 0:PACK].unsqueeze(1).to_broadcast([P, hi - lo, PACK]),
                op=mybir.AluOpType.mult)

        def scale_pairs(u, lo=0, hi=CW):
            V.tensor_tensor(
                out=h_of(u).rearrange("p (n h e) -> p n h e", h=2, e=2)[:, lo:hi, :, :],
                in0=step_of(act, u).rearrange("p (h n e) -> p n h e", h=2, e=2)[:, lo:hi, :, :],
                in1=hs_t[:, STEPS[u][0], 0:PACK].rearrange("p (h e) -> p h e", h=2).unsqueeze(1).to_broadcast([P, hi - lo, 2, 2]),
                op=mybir.AluOpType.mult)

        def half2(u, t, bank, slot):
            g = STEPS[u][0]
            cols = slice(H_AT[u], H_AT[u] + CW)
            ms = slice(W2_AT[g] + t * P, W2_AT[g] + (t + 1) * P)
            nc.tensor.matmul_mx(
                out=y_ps[bank][:, slot * CW:(slot + 1) * CW],
                lhsT=l2_q[:, ms].bitcast(FP8X4), lhsT_scale=l2_s[:, ms],
                rhs=l2_q[:, cols].bitcast(FP8X4), rhs_scale=l2_s[:, cols],
                start=True, stop=True)

        def evac(eng, bank, i, t0=0, t1=None):
            dst = y_sb[i][:, t0:t1, :].rearrange("p t n -> p (t n)")
            copy(eng, dst, y_ps[bank][:, 0:dst.shape[1]])

        def store(i, q=nc.sync):
            lo, hi, h0, h1 = STORES[i]
            q.dma_start(out=out_v[:, h0:h1, lo:hi], in_=y_sb[i][:])

        def window2(lo, t, bank):
            first = H_AT[7] + lo - 448
            words = slice(first, first + CW)
            ms = slice(W2_AT[0] + t * P, W2_AT[0] + (t + 1) * P)
            nc.tensor.matmul_mx(
                out=y_ps[bank][:, t * CW:(t + 1) * CW],
                lhsT=l2_q[:, ms].bitcast(FP8X4), lhsT_scale=l2_s[:, ms],
                rhs=l2_q[:, words].bitcast(FP8X4), rhs_scale=l2_s[:, words],
                start=True, stop=True)

        def evac_new(eng, bank, i):
            copy(eng, y_sb[i][:], y_ps[bank][:, 0:2 * CW].rearrange("p (t n) -> p t n", t=2)[:, :, CW // 2:CW])

        with tc.manual_schedule():
            load_w1(0)
            load_w1(1)
            load_x(0)
            load_x(1)
            load_x(2)
            load_x(3)
            load_hs()
            load_w2(1)
            load_w2(0)
            V.memset(warm[:, 0:1], 0.0)
            S.activation(out=warm[:, 1:2], in_=warm[:, 0:1], func=GELU)
            cast_w1(V, 0, 0, 4)
            cast_w1(V, 1, 0, 2)
            cast_w1(S, 1, 2, 4, 0, 80)
            cast_w1(V, 1, 2, 4, 80, 128)
            cast_x(S, 0, 48)
            cast_x(V, 48, 128)
            quant_w1(0, 2)
            quant_x(0, 1)
            layer1_first(0)
            quant_w1(2, 4)
            layer1_first(1)
            cast_x(S, 128, 256)
            cast_x(S, 256, 304)
            cast_x(V, 304, 384)
            quant_x(1, 2)
            layer1(2, 1)
            gelu_pair(0, 0)
            layer1(3, 0)
            gelu_pair(0, 1, 0, 64)
            gelu_pair(0, 1, 64, 128)
            quant_x(2, 3)
            cast_x(V, 384, 512)
            gelu(1, 0)
            scale_pairs(0, 0, 64)
            quant_x(3, 4)
            scale_pairs(0, 64, 128)
            layer1_two(5, 0, 4, 1)
            scale(1)
            gelu(2, 1)
            gelu(3, 0)
            layer1_two(6, 1, 7, 0)
            cast_w2(V, 1, 64, 256)
            cast_w2(S, 1, 0, 64)
            scale(2)
            scale(3)
            gelu(4, 1)
            cast_w2(S, 0, 0, 256)
            quant_l2(0, 512)
            half2(1, 0, 0, 0)
            half2(2, 0, 0, 1)
            half2(1, 1, 0, 2)
            half2(2, 1, 0, 3)
            gelu(5, 0)
            scale(4)
            quant_l2(512, 1024)
            quant_h(4)
            half2(0, 0, 1, 0)
            half2(3, 0, 1, 1)
            half2(4, 0, 1, 2)
            half2(0, 1, 2, 0)
            half2(3, 1, 2, 1)
            half2(4, 1, 2, 2)
            gelu(6, 1)
            evac(S, 0, 0)
            store(0)
            gelu(7, 0, 0, 64)
            gelu(7, 0, 64, 128)
            scale(5)
            evac(S, 1, 1)
            store(1)
            evac(S, 2, 2)
            store(2)
            scale(6)
            quant_h(5)
            half2(5, 0, 3, 0)
            half2(5, 1, 3, 1)
            scale(7, 0, 64)
            quant_h(6)
            half2(6, 0, 0, 0)
            half2(6, 1, 0, 1)
            evac(S, 3, 3)
            store(3)
            scale(7, 64, 128)
            quant_h(7, 0, 64)
            window2(384, 0, 1)
            window2(384, 1, 1)
            quant_h(7, 64, 128)
            window2(448, 0, 2)
            window2(448, 1, 2)
            evac(V, 0, 4)
            store(4)
            evac_new(V, 1, 5)
            store(5)
            evac_new(V, 2, 6)
            store(6)
